import numpy as np, ml_dtypes
CORES = [5,29,101,125,133,157,229,253]
N = 8
BF = ml_dtypes.bfloat16
def gentries(a):
    return np.ascontiguousarray(a.reshape(8, 16, -1).transpose(0, 2, 1)).reshape(8, -1)
def gtable(e):
    e = np.asarray(e); return np.ascontiguousarray(e.reshape(8, -1, 16).transpose(0, 2, 1)).reshape(128, -1).astype(np.int32)
LV, M, V, Q = 1, 2, 3, 2
C, S, T, U = 2048, 4096, 512, 320
def glists(e):
    return np.stack([gtable(e[r]) for r in range(N)])
def slots(rng):
    return np.argsort(rng.random((N, 8, N, C)), axis=-1)[..., :U]
def setup_inputs(rng):
    x = (0.125 + 0.875 * rng.random((N, 128, M * C), dtype=np.float32)).astype(BF)
    tr = (0.5 * rng.random((N, 128, 16 * (V + 1)), dtype=np.float32) ** 3).astype(BF)
    mp = rng.integers(0, C, (N, 8, (V - 1) * S)).astype(np.int32)
    rep = glists(rng.integers(0, S, (N, 8, (M - 1) * C)))
    uc = glists(slots(rng).reshape(N, 8, N * U))
    ps = glists(rng.integers(0, U, (N, 8, S)))
    return {"x": x, "tr": tr, "mp": mp, "rep": rep, "uc": uc, "ps": ps}
def setup_inputs_ends(rng):
    d = setup_inputs(rng)
    e = rng.integers(0, S, (N, 8, (M - 1) * C)); e = np.where(rng.random(e.shape) < 0.4, rng.choice(np.array([0, 1, S - 2, S - 1]), e.shape), e); e[:, :, 0] = S - 1; e[:, :, -1] = 0
    m = rng.integers(0, C, (N, 8, V - 1, S)); m = np.where(rng.random(m.shape) < 0.3, rng.choice(np.array([0, 1, C - 2, C - 1]), m.shape), m); m[..., 0] = C - 1; m[..., -1] = 0
    u = slots(rng); u[..., 0] = C - 1; u[..., -1] = 0
    p = rng.integers(0, U, (N, 8, N, T)); p = np.where(rng.random(p.shape) < 0.3, rng.choice(np.array([0, U - 1]), p.shape), p); p[..., 0] = U - 1; p[..., -1] = 0
    d["rep"] = glists(e); d["mp"] = m.reshape(N, 8, (V - 1) * S).astype(np.int32); d["uc"] = glists(u.reshape(N, 8, N * U)); d["ps"] = glists(p.reshape(N, 8, S)); return d
def setup_inputs_full(rng):
    d = setup_inputs(rng); p = np.concatenate([np.broadcast_to(np.arange(U), (N, 8, N, U)), rng.integers(0, U, (N, 8, N, T - U))], axis=-1)
    p = np.take_along_axis(p, np.argsort(rng.random(p.shape), axis=-1), -1)
    d["ps"] = glists(p.reshape(N, 8, S)); return d
def setup_inputs_alike(rng):
    d = setup_inputs(rng); a = int(rng.integers(0, N)); b = (a + 1) % N; c = (a + 2) % N
    e = gentries(d["rep"][a]); e[rng.integers(0, 8)] = rng.integers(0, S); d["rep"][a] = gtable(e)
    d["uc"][b] = gtable(np.repeat(rng.integers(0, C, (8, N)), U, axis=1))
    d["ps"][c] = gtable(np.repeat(rng.integers(0, U, (8, N)), T, axis=1)); return d
def setup_inputs_spread(rng):
    d = setup_inputs(rng); k = np.exp2(rng.integers(-2, 3, (N, 8, 1, C))) * (rng.random((N, 8, 1, C)) > 0.0625)
    x = d["x"].astype(np.float32).reshape(N, 8, 16, M * C); x[..., :C] *= k.astype(np.float32)
    d["x"] = x.reshape(N, 128, M * C).astype(BF); return d
def largest(x, t):
    P = t.astype(np.float64).reshape(N, 8, 16, V + 1, 16).transpose(0, 1, 3, 4, 2); top = x.reshape(N, 8, 16, M, C).max(axis=-1).astype(np.float64)
    X = [top[..., v] for v in range(M)]; seen = list(X)
    def times(p, v):
        return np.matmul(p, v[..., None])[..., 0]
    for k in range(M - 1):
        a, b = times(P[:, :, 2 * k], X[2 * k]), times(P[:, :, 2 * k + 1], X[2 * k + 1])
        X.append(a * b); seen += [a, b, a * b]
    Z = times(P[:, :, V - 1], X[V - 1]); seen.append(Z)
    for q in range(N):
        for k in range(Q):
            for a, b, c, e in ((0, 1, 2, 3), (0, 2, 1, 3), (0, 3, 1, 2)):
                h = Z[4 * k + a] * Z[4 * k + b]; l = Z[4 * k + c] * Z[4 * k + e]; w = times(P[q, :, V], l)
                seen += [h, l, w, np.sum(h * w, axis=-1)]
    return np.max(np.array([np.max(v) for v in seen]))
def check_inputs(d):
    bad = []
    try:
        x, t = np.asarray(d["x"]).astype(np.float32), np.asarray(d["tr"]).astype(np.float32)
        if not (np.isfinite(x).all() and (x >= 0).all() and (x <= 64).all()): bad.append("x")
        if not ((t >= 0) & (t <= 1)).all(): bad.append("tr")
        if not bad and not largest(x, t) < 2.0 ** 120: bad.append("size")
        for name, top in (("mp", C), ("rep", S), ("uc", C), ("ps", U)):
            a = np.asarray(d[name])
            if not ((a >= 0) & (a < top)).all(): bad.append(name)
    except Exception:
        bad.append("form")
    return bad
def reference(x, tr, mp, rep, uc, ps):
    z = np.zeros((N, 8, 16, C), np.float64); y = np.zeros((N, 8, Q, 3, T), np.float64)
    P = np.ascontiguousarray(tr.astype(np.float64).reshape(N, 8, 16, V + 1, 16).transpose(0, 1, 3, 4, 2))
    for r in range(N):
        leaf = x[r].astype(np.float64).reshape(8, 16, M, C); m = mp[r].reshape(8, V - 1, S); e = gentries(rep[r]).reshape(8, M - 1, C)
        for g in range(8):
            X = [leaf[g, :, v] for v in range(M)]
            for k in range(M - 1):
                a, b = 2 * k, 2 * k + 1; s = e[g, k]
                X.append((P[r, g, a] @ X[a])[:, m[g, a][s]] * (P[r, g, b] @ X[b])[:, m[g, b][s]])
            z[r, g] = P[r, g, V - 1] @ X[V - 1]
    u = [gentries(uc[r]).reshape(8, N, U) for r in range(N)]; p = [gentries(ps[r]).reshape(8, N, T) for r in range(N)]
    for q in range(N):
        w = P[q, :, V]; Z = []
        for r in range(N):
            c = np.take_along_axis(u[r][:, q], p[r][:, q], 1)
            Z.append(np.stack([z[r, g][:, c[g]] for g in range(8)]))
        for k in range(Q):
            for t, (a, b, c, d) in enumerate(((0, 1, 2, 3), (0, 2, 1, 3), (0, 3, 1, 2))):
                h = Z[4 * k + a] * Z[4 * k + b]; l = Z[4 * k + c] * Z[4 * k + d]
                y[q, :, k, t] = np.sum(h * np.matmul(w, l), axis=1)
    return {"y": y.reshape(N, 8, Q * 3 * T).astype(np.float32)}

@@ -1,0 +1,417 @@
+from concourse.bass import DstId, RemoteDMATransfer
+from concourse.mybir import AluOpType as ALU, ActivationFunctionType as ACT
+
+N, C, S, TT, U = 8, 2048, 4096, 512, 320
+UC = U // 16
+PC = TT // 16
+
+
+def _sb(n, d):
+    return ("sbuf", [128, n], d)
+
+
+SCRATCH = {
+    "xs": _sb(2 * C, "bfloat16"), "trz": _sb(80, "bfloat16"), "mpc": _sb(512, "int32"), "rep32": _sb(128, "int32"),
+    "rhl": _sb(256, "int32"), "ru16": _sb(256, "uint16"), "uc32": _sb(N * UC, "int32"), "uc16": _sb(N * UC, "uint16"),
+    "ps32": _sb(N * PC, "int32"), "psl": _sb(N * PC, "int32"), "po16": _sb(N * PC, "uint16"),
+    "ia": _sb(48, "int32"), "ia2": _sb(48, "int32"), "ib": _sb(32, "int32"), "ie": _sb(8, "int32"), "ie2": _sb(8, "int32"),
+    "ii": _sb(128, "int32"), "gm": _sb(32, "float32"), "bt": _sb(32, "float32"), "bdo": _sb(32, "uint16"),
+    "seg": _sb(8, "float32"), "sel": _sb(16, "float16"), "i16": _sb(128, "float16"), "i32": _sb(128, "float32"),
+    "bdb": _sb(256, "bfloat16"), "bdf": _sb(256, "float32"), "msk": _sb(C, "float32"), "g1": _sb(C, "float32"),
+    "g2": _sb(N * U, "float16"), "t1": _sb(768, "float16"), "l16": _sb(2 * N * UC, "uint16"), "px": _sb(2 * C, "float32"),
+    "ab": _sb(N * U, "float32"), "x2": _sb(N * U, "float32"), "zs": _sb(N * U, "float32"), "land": _sb(N * U, "float32"),
+    "xe": _sb(N * TT, "float32"), "ll": _sb(6 * TT, "float32"), "hh": _sb(TT, "float32"), "vv": _sb(6 * TT, "float32"),
+    "rs": _sb(192, "float32"), "ys": _sb(TT, "float32"), "acc": ("psum", [128, 4096], "float32"),
+}
+SEMAPHORES = (["cv", "cs", "cp", "cg", "sent", "psarr", "ydone"] + ["arr%d" % r for r in range(N)]
+              + ["d_rep", "d_mp", "d_tr", "d_uc", "d_ps", "d_x0", "d_x1", "d_x2", "d_x3"])
+
+OPT = {
+    "passes": [0, 3, 8],
+    "cuts": [0, 512, 1024, 1536, 2048],
+    "loads": "rep tr mp ps x0 uc x1 x2 x3", "on_s": ["tr"],
+    "own_at": 3, "own_due": 1, "relay_lag": 2.5,
+    "hsel": "f0 f1 f0 f1",
+    "tb": [7, 7, 0, 0],
+    "sched": """m0 bvb bvf m1 g0 pm0 g1 pm1 m2 m3 g2 phs0 g3 uc G2 pm2 phs1 G0 G1 phs2 G4 ta0 G3 tb0 phs3 phs4 pm3 phs5
+        tc0 G5 td0 phs7 phs6 a0 G7 a1 G6 ta1 x0 tb1 tc1 x1 td1 a2 zs0 a3 a4 x2 zv1 zs2 x3 a5 a6 x4 pown x5 x6 zv3 a7 zs4
+        po zs5 x7 zv6 e.x1 zs7 e.x2 e.a1 lg3 lg2 lg1 h e.z1 e.z2 u.x2 v.x3 r.x3 p1 v.x2 r.x2 u.x1 lp3 v.x1 e.z3 p2 e.a2
+        lp2 u.z3 lp1 r.x1 u.z2 v.z3 v.z2 r.z3 r.z2""".split(),
+    "tail": "u.z1.0.2 u.z1.2.2 v.z1.0.2 r.z1.0.2 v.z1.2.2 r.z1.2.2 Rs02 Rv22 T0 T1 T2 T3 Ys02 Yv22",
+}
+
+
+def bits(engines):
+    m = 0
+    for e in engines:
+        m |= 1 << e
+    return m
+
+
+def block_order(cores, r, topo):
+    near = [r ^ m for m in range(1, 4)]
+    far = [r ^ m for m in range(4, 8)]
+    def key(q):
+        return 1 if topo.may_write(cores[r], cores[q]) else 0
+    o = sorted(near, key=key) + sorted(far, key=key)
+    return o[:OPT["own_at"]] + [r] + o[OPT["own_at"]:]
+
+
+def helpers_of(cores, r, topo):
+    me = cores[r]
+    relayed = [q for q in block_order(cores, r, topo) if q != r and not topo.may_write(me, cores[q])]
+    able = [c for c in topo.cores_of(me) if c not in cores and all(topo.may_write(c, cores[q]) for q in relayed)]
+    other = [c for c in able if topo.die(c) != topo.die(me)]
+    near = [c for c in able if topo.die(c) == topo.die(me)]
+    use = [(other if w[0] == "f" else near)[int(w[1])] for w in OPT["hsel"].split()]
+    return {q: (use[i], use[:i].count(use[i])) for i, q in enumerate(relayed)}
+
+
+def split_engines(engines, k):
+    sizes = [1] * k
+    while True:
+        i = sizes.index(min(sizes))
+        if sum(sizes) + sizes[i] > len(engines):
+            break
+        sizes[i] *= 2
+    out, a = [], 0
+    for s in sizes:
+        out.append(engines[a:a + s])
+        a += s
+    return out
+
+
+def ps_plan(cores, r, topo):
+    me = cores[r]
+    hs = helpers_of(cores, r, topo)
+    helpers = sorted(set(h for h, k in hs.values()))
+    direct = [q for q in range(N) if q != r and q not in hs]
+    rel = sorted(hs)
+    per = len(rel) // len(helpers)
+    via = {h: rel[per * i:per * (i + 1)] for i, h in enumerate(helpers)}
+    width = max(max(v) - min(v) + 1 for v in via.values())
+    first = [(h, e, min(min(via[h]), N - width), width)
+             for h, e in zip(helpers, split_engines(topo.engines(me, helpers[0]), len(helpers)))]
+    straight = list(zip(direct, split_engines(topo.engines(me, cores[direct[0]]), len(direct))))
+    second = {h: list(zip(via[h], split_engines(topo.engines(h, cores[via[h][0]]), len(via[h])))) for h in helpers}
+    return first, straight, second
+
+
+def z_engines(cores, r, q, topo):
+    hs = helpers_of(cores, r, topo)
+    return topo.engines(cores[r], hs[q][0] if q in hs else cores[q])
+
+
+def helper_program(g, core, T, topo, r):
+    cores = T.cores
+    hs = helpers_of(cores, r, topo)
+    first, straight, second = ps_plan(cores, r, topo)
+    sent = 0
+    g.wait_ge(T.sem.psarr, sum(len(f[1]) for f in first if f[0] == core))
+    trs = []
+    for q, e in second[core]:
+        rid, pid = topo.addr(cores[q], core)
+        trs.append(RemoteDMATransfer(dst_ids=[DstId(rid=rid, pnc=pid)], dma_engine_mask=bits(e), remote_sem=T.sem.psarr,
+                                     src=T.ps32[:, PC * q:PC * (q + 1)], dst=T.psl[:, PC * (r ^ q):PC * ((r ^ q) + 1)]))
+        sent += len(e)
+    g.remote_dma_fused(trs, local_sem=T.sem.sent)
+    for q in sorted([q for q in hs if hs[q][0] == core], key=lambda q: hs[q][1]):
+        k = hs[q][1]
+        g.wait_ge(T.sem["arr%d" % k], len(z_engines(cores, r, q, topo)))
+        rid, pid = topo.addr(cores[q], core)
+        g.remote_dma(T.land[:, U * r:U * (r + 1)], T.land[:, U * k:U * (k + 1)], T.sem["arr%d" % r], T.sem.sent,
+                     pid, rid, topo.mask(core, cores[q]))
+        sent += len(topo.engines(core, cores[q]))
+    g.wait_ge(T.sem.sent, sent)
+
+
+def rank_program(g, core, T, topo):
+    cores = T.cores
+    rank = T.rank_of(core)
+    if rank is None:
+        for r in range(N):
+            if core in topo.cores_of(cores[r]) and core in [h for h, k in helpers_of(cores, r, topo).values()]:
+                helper_program(g, core, T, topo, r)
+        return
+    queue = {"v": g.vector, "s": g.scalar, "p": g.tensor, "g": g, "y": g.sync}
+    esem = {"v": "cv", "s": "cs", "p": "cp", "g": "cg"}
+    total = {}
+    waited = {k: {} for k in queue}
+    wrote, read = {}, {}
+
+    def wait(q, sem, n):
+        if waited[q].get(sem, 0) < n:
+            queue[q].wait_ge(T.sem[sem], n)
+            waited[q][sem] = n
+
+    def order(q, rd, wr):
+        mine = esem.get(q)
+        need = {}
+        def add(s, n):
+            need[s] = max(need.get(s, 0), n)
+        for t in rd:
+            add(*wrote[t])
+            if t[0] == "B":
+                for s, n in read.get(t, {}).items():
+                    if s != mine:
+                        add(s, n)
+        for t in wr:
+            if t in wrote and wrote[t][0] != mine:
+                add(*wrote[t])
+            for s, n in read.get(t, {}).items():
+                if s != mine:
+                    add(s, n)
+        for s in need:
+            wait(q, s, need[s])
+
+    def op(q, calls, rd, wr):
+        order(q, rd, wr)
+        s = esem[q]
+        for c in calls:
+            c().then_inc(T.sem[s], 1)
+            total[s] = total.get(s, 0) + 1
+        for t in rd:
+            read.setdefault(t, {})[s] = total[s]
+        for t in wr:
+            wrote[t] = (s, total[s])
+            read[t] = {}
+
+    V, A, P = g.vector, g.scalar, g.tensor
+    acc = T.acc
+    def bank(b, a=0, n=512):
+        return acc[:, 512 * b + a:512 * b + a + n]
+    def copy(q, o, i, rd, wr):
+        op(q, [(lambda: A.activation(o, i, ACT.Copy)) if q == "s" else (lambda: V.tensor_copy(o, i))], rd, wr)
+
+    blocks = block_order(cores, rank, topo)
+    hs = helpers_of(cores, rank, topo)
+
+    total["psarr"] = 0
+    for r in range(N):
+        if r != rank:
+            h = helpers_of(cores, r, topo)
+            src = h[rank][0] if rank in h else cores[r]
+            total["arr%d" % r] = len(topo.engines(src, core))
+            wrote["land%d" % r] = ("arr%d" % r, total["arr%d" % r])
+            first, straight, second = ps_plan(cores, r, topo)
+            total["psarr"] += sum(len(e) for q, e in straight if q == rank)
+            total["psarr"] += sum(len(e) for c in second for q, e in second[c] if q == rank)
+    wrote["psl"] = ("psarr", total["psarr"])
+
+    sides = {"rep": (T.rep32[:], T.rep[:]), "mp": (T.mpc[:], T.mp[:]), "tr": (T.trz[:, 0:64], T.tr[:]),
+             "uc": (T.uc32[:], T.uc[:]), "ps": (T.ps32[:], T.ps[:])}
+    for j in range(4):
+        sides["x%d" % j] = (T.xs[:, 1024 * j:1024 * (j + 1)], T.x[:, 1024 * j:1024 * (j + 1)])
+    for name in OPT["loads"].split():
+        queue["s" if name in OPT["on_s"] else "y"].dma_start(*sides[name]).then_inc(T.sem["d_" + name], 16)
+        total["d_" + name] = 16
+        wrote["d_" + name] = ("d_" + name, 16)
+
+    op("g", [lambda: g.iota(T.ie[:], [[-1, 8]], 8, 1)], [], ["ie"])
+    op("g", [lambda: g.iota(T.ia[:, 0:32], [[0, 4], [-16, 8]], 128, 1)], [], ["ia0"])
+    op("g", [lambda: g.iota(T.ib[:], [[16, 4], [-16, 8]], -64, 1)], [], ["ib"])
+    op("g", [lambda: g.iota(T.ia[:, 32:48], [[-16, 2], [-32, 8]], 128, 2)], [], ["ia1"])
+    op("g", [lambda: g.iota(T.ii[:], [[-1, 128]], 0, 1)], [], ["ii"])
+    op("v", [lambda: V.memset(T.trz[:, 64:80], 0.0)], [], ["trz"])
+    op("v", [lambda: V.tensor_scalar(T.ie2[:], T.ie[:], 7, None, ALU.bitwise_and)], ["ie"], ["ie2"])
+    op("v", [lambda: V.tensor_scalar(T.ia2[:], T.ia[:], 4, None, ALU.arith_shift_right)], ["ia0", "ia1"], ["ia2"])
+    op("v", [lambda: V.tensor_scalar(T.seg[:], T.ie2[:], 0.0, None, ALU.is_equal)], ["ie2"], ["seg"])
+    op("v", [lambda: V.tensor_scalar(T.gm[:], T.ia2[:, 0:32], 8.0, None, ALU.is_equal)], ["ia2"], ["gm"])
+    op("v", [lambda: V.tensor_scalar(T.sel[:], T.ia2[:, 32:48], 8.0, None, ALU.is_equal)], ["ia2"], ["sel"])
+    op("v", [lambda: V.tensor_tensor(T.bt[:], T.ib[:], T.gm[:], ALU.mult)], ["ib", "gm"], ["bt"])
+    op("v", [lambda: V.tensor_scalar(T.i16[:], T.ii[:], 0.0, None, ALU.is_equal)], ["ii"], ["i16"])
+    op("v", [lambda: V.tensor_scalar(T.bdo[:], T.bt[:], 64.0, None, ALU.add)], ["bt"], ["bdo"])
+    op("v", [lambda: V.tensor_scalar(T.i32[:], T.ii[:], 0.0, None, ALU.is_equal)], ["ii"], ["i32"])
+
+    order("g", ["d_ps"], [])
+    total["sent"] = 0
+    first, straight, second = ps_plan(cores, rank, topo)
+    for plan in ([(c, e, q0, n, T.ps32, q0) for c, e, q0, n in first],
+                 [(cores[q], e, q, 1, T.psl, q ^ rank) for q, e in straight]):
+        trs = []
+        for c, e, q0, n, to, k in plan:
+            rid, pid = topo.addr(c, core)
+            trs.append(RemoteDMATransfer(dst_ids=[DstId(rid=rid, pnc=pid)], dma_engine_mask=bits(e), remote_sem=T.sem.psarr,
+                                         src=T.ps32[:, PC * q0:PC * (q0 + n)], dst=to[:, PC * k:PC * (k + n)]))
+            total["sent"] += len(e)
+        g.remote_dma_fused(trs, local_sem=T.sem.sent)
+
+    op("v", [lambda: V.tensor_scalar(T.rhl[:, 0:128], T.rep32[:], 9, None, ALU.arith_shift_right)], ["d_rep"], ["rh"])
+    op("v", [lambda: V.tensor_scalar(T.rhl[:, 128:256], T.rep32[:], 511, None, ALU.bitwise_and)], ["d_rep"], ["rl"])
+    copy("v", T.ru16[:, 0:128], T.rhl[:, 0:128], ["rh"], ["rh16"])
+    copy("v", T.ru16[:, 128:256], T.rhl[:, 128:256], ["rl"], ["rl16"])
+    cuts, passes = OPT["cuts"], OPT["passes"]
+    G1 = ["g1_%d" % i for i in range(len(cuts) - 1)]
+    def mask_op(i):
+        a, b = cuts[i], cuts[i + 1]
+        copy("s", T.msk[:, a:b], T.seg[:, 0:8].indirect(T.ru16[:, a // 16:b // 16]), ["seg", "rh16"], ["msk%d" % i])
+    def g1_op(i):
+        a, b = cuts[i], cuts[i + 1]
+        op("v", [lambda: V.tensor_tensor(T.g1[:, a:b], T.mpc[:, 0:512].indirect(T.ru16[:, 128 + a // 16:128 + b // 16]),
+                                         T.msk[:, a:b], ALU.mult)], ["d_mp", "rl16", "msk%d" % i], ["g1_%d" % i])
+
+    pxb = [0, 2, 6, 0]
+    def px_mm(j):
+        v, b = j // 2, pxb[j]
+        op("p", [lambda k=k: P.matmul(bank(b + k), T.bdb[:, 128 * v:128 * (v + 1)],
+                                      T.xs[:, 1024 * j + 512 * k:1024 * j + 512 * (k + 1)], True, True) for k in range(2)],
+           ["bdb", "d_x%d" % j], ["B%d" % b, "B%d" % (b + 1)])
+    def px_copy(q, j, h=None):
+        b = pxb[j]
+        if h is None:
+            copy(q, T.px[:, 1024 * j:1024 * (j + 1)], bank(b, 0, 1024), ["B%d" % b, "B%d" % (b + 1)], ["px%d0" % j, "px%d1" % j])
+        else:
+            copy(q, T.px[:, 1024 * j + 512 * h:1024 * j + 512 * (h + 1)], bank(b + h), ["B%d" % (b + h)], ["px%d%d" % (j, h)])
+
+    def g2_op(k):
+        q = blocks[k]
+        copy("v", T.g2[:, U * k:U * (k + 1)], T.g1[:, 0:C].indirect(T.uc16[:, UC * q:UC * (q + 1)]), G1 + ["uc16"], ["g2_%d" % k])
+    def span(i):
+        return passes[i], passes[i + 1], UC * (passes[i + 1] - passes[i])
+    def turn1(i):
+        k0, k1, n = span(i)
+        op("p", [lambda b=b: P.matmul(acc[0:n, 2048 + b:2048 + 256:16], T.g2[:, U * k0 + b:U * k1:16], T.sel[:], True, True)
+                 for b in range(16)], ["sel"] + ["g2_%d" % k for k in range(k0, k1)], ["B4"])
+    def turn1_copy(i):
+        k0, k1, n = span(i)
+        copy("v", T.t1[0:n, 256 * i:256 * (i + 1)], acc[0:n, 2048:2048 + 256], ["B4"], ["t1_%d" % i])
+    def turn2(i):
+        k0, k1, n = span(i)
+        op("p", [lambda v=v: P.matmul(bank(5, n * v, n), T.t1[0:n, 256 * i + 128 * v:256 * i + 128 * (v + 1)],
+                                      T.i16[0:n, 0:n], True, True) for v in range(2)], ["t1_%d" % i, "i16"], ["B5"])
+    def turn2_copy(i):
+        k0, k1, n = span(i)
+        copy("v", T.l16[:, 2 * UC * k0:2 * UC * k1], bank(5, 0, 2 * n), ["B5"], ["l16_%d" % i])
+    def lists(k, v):
+        i = [j for j in range(len(passes) - 1) if passes[j] <= k < passes[j + 1]][0]
+        k0, k1, n = span(i)
+        a = 2 * UC * k0 + n * v + UC * (k - k0)
+        return T.l16[:, a:a + UC], "l16_%d" % i
+
+    zbank = [6, 7, 2, 3]
+    def a_op(k):
+        ap, t = lists(k, 0)
+        copy("s", T.ab[:, U * k:U * (k + 1)], T.px[:, 0:C].indirect(ap), [t, "px00", "px01", "px10", "px11"], ["ab%d" % k])
+    def x2_op(k):
+        ap, t = lists(k, 1)
+        op("v", [lambda: V.tensor_tensor(T.x2[:, U * k:U * (k + 1)], T.px[:, C:2 * C].indirect(ap), T.ab[:, U * k:U * (k + 1)],
+                                         ALU.mult)], [t, "px20", "px21", "px30", "px31", "ab%d" % k], ["x2_%d" % k])
+        b = zbank[k % 4]
+        op("p", [lambda: P.matmul(bank(b, 0, U), T.bdf[:, 0:128], T.x2[:, U * k:U * (k + 1)], True, True)],
+           ["bdf", "x2_%d" % k], ["B%d" % b])
+    def z_op(eng, k):
+        q = blocks[k]
+        b = zbank[k % 4]
+        o = T.land[:, U * q:U * (q + 1)] if q == rank else T.zs[:, U * k:U * (k + 1)]
+        copy(eng, o, bank(b, 0, U), ["B%d" % b], ["land%d" % q if q == rank else "zs%d" % k])
+        if q == rank:
+            return
+        order("g", ["zs%d" % k], [])
+        dst, slot = hs[q] if q in hs else (cores[q], rank)
+        rid, pid = topo.addr(dst, core)
+        e = z_engines(cores, rank, q, topo)
+        g.remote_dma(T.land[:, U * slot:U * (slot + 1)], o, T.sem["arr%d" % slot], T.sem.sent, pid, rid, bits(e))
+        total["sent"] += len(e)
+
+    def due(r):
+        if r == rank:
+            return OPT["own_due"]
+        return block_order(cores, r, topo).index(rank) + (OPT["relay_lag"] if rank in helpers_of(cores, r, topo) else 0)
+    def win(r):
+        return T.land[:, U * r:U * (r + 1)].indirect(T.po16[:, PC * (r ^ rank):PC * ((r ^ rank) + 1)])
+    def po(r):
+        return "po_own" if r == rank else "po16"
+    def xe(r):
+        return T.xe[:, TT * r:TT * (r + 1)]
+    def expand(r):
+        copy("s", xe(r), win(r), ["land%d" % r, po(r)], ["xe%d" % r])
+    def to_psum(r, b):
+        copy("s", bank(b), xe(r), ["xe%d" % r], ["B%d" % b])
+    def kt(y):
+        return 3 * (y // 4) + y % 4 - 1
+    def col(buf, y, a=0, n=TT):
+        return buf[:, TT * kt(y) + a:TT * kt(y) + a + n]
+    wb = {}
+    def w_mm(y, b):
+        wb[y] = b
+        op("p", [lambda: P.matmul(bank(b), T.bdf[:, 128:256], col(T.ll, y), True, True)], ["bdf", "l%d" % y], ["B%d" % b])
+    def l_gather(y, a, b, w):
+        op("v", [lambda: V.tensor_tensor(col(T.ll, y), win(a), xe(b), ALU.mult)], ["land%d" % a, po(a), "xe%d" % b], ["l%d" % y])
+        w_mm(y, w)
+    def l_psum(y, a, b, w):
+        op("v", [lambda: V.tensor_tensor(col(T.ll, y), xe(a), bank(b), ALU.mult)], ["xe%d" % a, "B%d" % b], ["l%d" % y])
+        w_mm(y, w)
+    def u_op(y, a=0, n=TT):
+        b = wb[y]
+        op("v", [lambda: V.tensor_tensor(bank(b, a, n), xe(y)[:, a:a + n], bank(b, a, n), ALU.mult)],
+           ["xe%d" % y, "B%d" % b], ["B%d" % b])
+    def v_op(y, a=0, n=TT):
+        b = wb[y]
+        src, tok = (T.hh, "hh") if y == role["x3"] and "h" in OPT["sched"] else (xe(4 * (y // 4)), "xe%d" % (4 * (y // 4)))
+        op("v", [lambda: V.tensor_tensor(col(T.vv, y, a, n), src[:, a:a + n], bank(b, a, n), ALU.mult)],
+           [tok, "B%d" % b], ["v%d_%d" % (y, h) for h in range(a // 128, (a + n) // 128)])
+    def rcol(c):
+        return 512 * (5 + c // 2) + 48 * (c % 2)
+    def r_mm(y, a=0, n=TT):
+        for c in range(a // 128, (a + n) // 128):
+            op("p", [lambda: P.matmul(acc[:, rcol(c) + kt(y):rcol(c) + 48:6], col(T.vv, y, 128 * c, 128), T.gm[:, 0:8], True, True)],
+               ["gm", "v%d_%d" % (y, c)], ["B%d" % (5 + c // 2)])
+    def r_copy(q, c, n):
+        copy(q, T.rs[:, 48 * c:48 * (c + n)], acc[:, rcol(c):rcol(c) + 48 * n], ["B%d" % (5 + c // 2)],
+             ["rs%d" % k for k in range(c, c + n)])
+    tb = OPT["tb"]
+    def tcol(c):
+        return 512 * tb[c] + 128 * c
+    def t_mm(c):
+        op("p", [lambda: P.transpose(acc[0:48, tcol(c):tcol(c) + 128], T.rs[:, 48 * c:48 * (c + 1)], T.i32[:])],
+           ["rs%d" % c, "i32"], ["B%d" % tb[c]])
+    def y_copy(q, c, n):
+        copy(q, T.ys[0:48, 128 * c:128 * (c + n)], acc[0:48, tcol(c):tcol(c) + 128 * n], ["B%d" % tb[c]],
+             ["ys%d" % k for k in range(c, c + n)])
+
+    a1 = 4 * (rank // 4)
+    a2 = 4 - a1
+    x1, x2, x3 = sorted(range(a1 + 1, a1 + 4), key=due)
+    z1, z2, z3 = sorted(range(a2 + 1, a2 + 4), key=due)
+    role = {"a1": a1, "a2": a2, "x1": x1, "x2": x2, "x3": x3, "z1": z1, "z2": z2, "z3": z3}
+    def diag(q, out, a, name):
+        copy(q, out, T.trz[:, 0:80].indirect(T.bdo[:, a:a + 16]), ["d_tr", "trz", "bdo"], [name])
+    step = {
+        "bdb": lambda: diag("s", T.bdb[:], 0, "bdb"), "bdf": lambda: diag("s", T.bdf[:], 16, "bdf"),
+        "bvb": lambda: diag("v", T.bdb[:], 0, "bdb"), "bvf": lambda: diag("v", T.bdf[:], 16, "bdf"),
+        "uc": lambda: copy("v", T.uc16[:], T.uc32[:], ["d_uc"], ["uc16"]),
+        "po": lambda: copy("v", T.po16[:, PC:], T.psl[:, PC:], ["psl"], ["po16"]),
+        "pown": lambda: copy("v", T.po16[:, 0:PC], T.ps32[:, PC * rank:PC * (rank + 1)], ["d_ps"], ["po_own"]),
+        "h": lambda: op("v", [lambda: V.tensor_tensor(T.hh[:], win(x3), xe(a1), ALU.mult)],
+                        ["land%d" % x3, po(x3), "xe%d" % a1], ["hh"]),
+        "lg3": lambda: l_gather(x3, x2, x1, 2), "lg2": lambda: l_gather(x2, x3, x1, 3), "lg1": lambda: l_gather(x1, x3, x2, 4),
+        "p1": lambda: to_psum(z1, 7), "p2": lambda: to_psum(z2, 1),
+        "lp3": lambda: l_psum(z3, z2, 7, 2), "lp2": lambda: l_psum(z2, z3, 7, 3), "lp1": lambda: l_psum(z1, z3, 1, 4),
+    }
+    by_number = {"m": mask_op, "g": g1_op, "G": g2_op, "pm": px_mm, "ta": turn1, "tb": turn1_copy, "tc": turn2, "td": turn2_copy,
+                 "a": a_op, "x": x2_op, "zs": lambda k: z_op("s", k), "zv": lambda k: z_op("v", k),
+                 "pcs": lambda j: px_copy("s", j), "pcv": lambda j: px_copy("v", j),
+                 "phs": lambda j: px_copy("s", j // 2, j % 2), "phv": lambda j: px_copy("v", j // 2, j % 2)}
+    by_role = {"e": expand, "u": u_op, "v": v_op, "r": r_mm}
+    for s in OPT["sched"] + OPT["tail"].split():
+        if s in step:
+            step[s]()
+        elif s.count(".") == 3:
+            f, y, a, n = s.split(".")
+            by_role[f](role[y], 128 * int(a), 128 * int(n))
+        elif "." in s:
+            by_role[s.split(".")[0]](role[s.split(".")[1]])
+        elif s[0] in "RY":
+            (r_copy if s[0] == "R" else y_copy)(s[1], int(s[2]), int(s[3]))
+        elif s[0] == "T":
+            t_mm(int(s[1]))
+        else:
+            by_number[s[:-1]](int(s[-1]))
+
+    order("y", ["ys0", "ys1", "ys2", "ys3"], [])
+    g.sync.dma_start(T.y[:], T.ys[0:48, :]).then_inc(T.sem.ydone, 16)
+    total["ydone"] = 16
+    for s in total:
+        if s != "ydone" and max(waited[q].get(s, 0) for q in waited) < total[s]:
+            wait("g", s, total[s])
+    wait("y", "ydone", 16)

@@ -11,33 +11,30 @@ def _sb(n, d):
 
 
 SCRATCH = {
-    "xs": _sb(2 * C, "bfloat16"), "trz": _sb(80, "bfloat16"), "mpc": _sb(512, "int32"), "rep32": _sb(128, "int32"),
-    "rhl": _sb(256, "int32"), "ru16": _sb(256, "uint16"), "uc32": _sb(N * UC, "int32"), "uc16": _sb(N * UC, "uint16"),
+    "xs": _sb(2 * C, "bfloat16"), "trz": _sb(80, "bfloat16"), "mw": _sb(S, "int32"), "rep32": _sb(128, "int32"),
+    "r16": _sb(128, "uint16"), "uc32": _sb(N * UC, "int32"), "uc16": _sb(N * UC, "uint16"),
     "ps32": _sb(N * PC, "int32"), "psl": _sb(N * PC, "int32"), "po16": _sb(N * PC, "uint16"),
-    "ia": _sb(48, "int32"), "ia2": _sb(48, "int32"), "ib": _sb(32, "int32"), "ie": _sb(8, "int32"), "ie2": _sb(8, "int32"),
-    "ii": _sb(128, "int32"), "gm": _sb(32, "float32"), "bt": _sb(32, "float32"), "bdo": _sb(32, "uint16"),
-    "seg": _sb(8, "float32"), "sel": _sb(16, "float16"), "i16": _sb(128, "float16"), "i32": _sb(128, "float32"),
-    "bdb": _sb(256, "bfloat16"), "bdf": _sb(256, "float32"), "msk": _sb(C, "float32"), "g1": _sb(C, "float32"),
-    "g2": _sb(N * U, "float16"), "t1": _sb(768, "float16"), "l16": _sb(2 * N * UC, "uint16"), "px": _sb(2 * C, "float32"),
-    "ab": _sb(N * U, "float32"), "x2": _sb(N * U, "float32"), "zs": _sb(N * U, "float32"), "land": _sb(N * U, "float32"),
-    "xe": _sb(N * TT, "float32"), "ll": _sb(6 * TT, "float32"), "hh": _sb(TT, "float32"), "vv": _sb(6 * TT, "float32"),
-    "rs": _sb(192, "float32"), "ys": _sb(TT, "float32"), "acc": ("psum", [128, 4096], "float32"),
+    "ia": _sb(32, "int32"), "ia2": _sb(32, "int32"), "ib": _sb(32, "int32"), "ic": _sb(36, "int32"), "ic2": _sb(36, "int32"),
+    "ie": _sb(288, "int32"), "ii": _sb(128, "int32"), "gm": _sb(32, "float32"), "bt": _sb(32, "float32"),
+    "bdo": _sb(32, "uint16"), "ones": _sb(36, "float32"), "sel": _sb(288, "float16"), "i32": _sb(128, "float32"),
+    "bdb": _sb(256, "bfloat16"), "bdw": _sb(256, "float32"), "g1": _sb(C, "float32"), "g2": _sb(N * U, "float16"),
+    "l16": _sb(2 * N * UC, "uint16"), "px": _sb(2 * C, "float32"), "ab": _sb(N * U, "float32"), "x2": _sb(N * U, "float32"),
+    "zs": _sb(N * U, "float32"), "land": _sb(N * U, "float32"), "raw": _sb(128 + U, "float32"), "lraw": _sb(128 + U, "float32"),
+    "xe": _sb(N * TT, "float32"), "ll": _sb(6 * TT, "float32"), "vv": _sb(6 * TT, "float32"),
+    "rs": _sb(192, "float32"), "ys": _sb(384, "float32"), "acc": ("psum", [128, 4096], "float32"),
 }
 SEMAPHORES = (["cv", "cs", "cp", "cg", "sent", "psarr", "ydone"] + ["arr%d" % r for r in range(N)]
               + ["d_rep", "d_mp", "d_tr", "d_uc", "d_ps", "d_x0", "d_x1", "d_x2", "d_x3"])
 
 OPT = {
-    "passes": [0, 3, 8],
-    "cuts": [0, 512, 1024, 1536, 2048],
-    "loads": "rep tr mp ps x0 uc x1 x2 x3", "on_s": ["tr"],
-    "own_at": 3, "own_due": 1, "relay_lag": 2.5,
-    "hsel": "f0 f1 f0 f1",
-    "tb": [7, 7, 0, 0],
-    "sched": """m0 bvb bvf m1 g0 pm0 g1 pm1 m2 m3 g2 phs0 g3 uc G2 pm2 phs1 G0 G1 phs2 G4 ta0 G3 tb0 phs3 phs4 pm3 phs5
-        tc0 G5 td0 phs7 phs6 a0 G7 a1 G6 ta1 x0 tb1 tc1 x1 td1 a2 zs0 a3 a4 x2 zv1 zs2 x3 a5 a6 x4 pown x5 x6 zv3 a7 zs4
-        po zs5 x7 zv6 e.x1 zs7 e.x2 e.a1 lg3 lg2 lg1 h e.z1 e.z2 u.x2 v.x3 r.x3 p1 v.x2 r.x2 u.x1 lp3 v.x1 e.z3 p2 e.a2
-        lp2 u.z3 lp1 r.x1 u.z2 v.z3 v.z2 r.z3 r.z2""".split(),
-    "tail": "u.z1.0.2 u.z1.2.2 v.z1.0.2 r.z1.0.2 v.z1.2.2 r.z1.2.2 Rs02 Rv22 T0 T1 T2 T3 Ys02 Yv22",
+    "fill": [384, 1536, 4, 640],
+    "loads": "rep uc x0 mp x1 x2 x3 ps",
+    "via": "f0n0 f1n1 F0 F1",
+    "sched": """rv ucv bdb pm0 p2v cst ws pm1 pv0 pm3 pm2 ps1 gs1 pm5 sel pm4 gv0 Gs1 Gv0 pm6 pm7 pv4 ps3 t0 ps2 pv6 ls0
+        t1 ps7 Gs2 pv5 Gs3 av.r1 lv1 b.r1 zs.r1 wts ov av.r2 t2 b.r2 av.e1 lv2 t3 as.e2 as.e3 zs.r2 ls3 b.e2 av.r3
+        as.r4 b.r3 zs.e2 b.e1 b.r4 as.e4 zs.r3 b.e3 pos xs.e1 b.e4 zv.r4 xs.e2 xs.r2 xv.r1 m.1a m.1e m.1b u.1a u.1e
+        zs.e4 xs.e3 xs.r3 xs.e4 v.1a u.1b v.1e v.1b m.2a m.2e u.2a fs.1 xs.r4 m.2b ys.1 u.2e v.2a v.2e u.2b fv.2 ys.2
+        end""".split(),
 }
 
 
@@ -46,25 +43,6 @@ def bits(engines):
     for e in engines:
         m |= 1 << e
     return m
-
-
-def block_order(cores, r, topo):
-    near = [r ^ m for m in range(1, 4)]
-    far = [r ^ m for m in range(4, 8)]
-    def key(q):
-        return 1 if topo.may_write(cores[r], cores[q]) else 0
-    o = sorted(near, key=key) + sorted(far, key=key)
-    return o[:OPT["own_at"]] + [r] + o[OPT["own_at"]:]
-
-
-def helpers_of(cores, r, topo):
-    me = cores[r]
-    relayed = [q for q in block_order(cores, r, topo) if q != r and not topo.may_write(me, cores[q])]
-    able = [c for c in topo.cores_of(me) if c not in cores and all(topo.may_write(c, cores[q]) for q in relayed)]
-    other = [c for c in able if topo.die(c) != topo.die(me)]
-    near = [c for c in able if topo.die(c) == topo.die(me)]
-    use = [(other if w[0] == "f" else near)[int(w[1])] for w in OPT["hsel"].split()]
-    return {q: (use[i], use[:i].count(use[i])) for i, q in enumerate(relayed)}
 
 
 def split_engines(engines, k):
@@ -81,30 +59,54 @@ def split_engines(engines, k):
     return out
 
 
+def peers(cores, r, topo):
+    others = [r ^ m for m in range(1, N)]
+    direct = [q for q in others if topo.may_write(cores[r], cores[q])]
+    return direct, [q for q in others if q not in direct]
+
+
+def helpers(cores, r, topo):
+    me = cores[r]
+    able = [c for c in topo.cores_of(me)
+            if c not in cores and all(topo.may_write(c, cores[q]) for q in peers(cores, r, topo)[1])]
+    return [c for c in able if topo.die(c) != topo.die(me)], [c for c in able if topo.die(c) == topo.die(me)]
+
+
+def block_plan(cores, r, topo):
+    me = cores[r]
+    direct, handed = peers(cores, r, topo)
+    far, near = helpers(cores, r, topo)
+    plan = {q: [(0, U, cores[q], r, topo.engines(me, cores[q]))] for q in direct}
+    seen = {}
+    for q, w in zip(handed, OPT["via"].split()):
+        hs = [(far if w[i] in "fF" else near)[int(w[i + 1])] for i in range(0, len(w), 2)]
+        free = topo.engines(me, hs[0])
+        if w[0].isupper():
+            free = [e for e in free if e not in topo.engines(me, cores[direct[0]])]
+        n = U // len(hs)
+        plan[q] = []
+        for i, (c, e) in enumerate(zip(hs, split_engines(free, len(hs)))):
+            plan[q].append((n * i, n, c, seen.get(c, 0), e))
+            seen[c] = seen.get(c, 0) + 1
+    return plan
+
+
 def ps_plan(cores, r, topo):
     me = cores[r]
-    hs = helpers_of(cores, r, topo)
-    helpers = sorted(set(h for h, k in hs.values()))
-    direct = [q for q in range(N) if q != r and q not in hs]
-    rel = sorted(hs)
-    per = len(rel) // len(helpers)
-    via = {h: rel[per * i:per * (i + 1)] for i, h in enumerate(helpers)}
+    direct, handed = peers(cores, r, topo)
+    hs = sorted(set(t[2] for ts in block_plan(cores, r, topo).values() for t in ts if t[2] not in cores))
+    rel = sorted(handed)
+    per = len(rel) // len(hs)
+    via = {h: rel[per * i:per * (i + 1)] for i, h in enumerate(hs)}
     width = max(max(v) - min(v) + 1 for v in via.values())
-    first = [(h, e, min(min(via[h]), N - width), width)
-             for h, e in zip(helpers, split_engines(topo.engines(me, helpers[0]), len(helpers)))]
+    first = [(h, e, min(min(via[h]), N - width), width) for h, e in zip(hs, split_engines(topo.engines(me, hs[0]), len(hs)))]
     straight = list(zip(direct, split_engines(topo.engines(me, cores[direct[0]]), len(direct))))
-    second = {h: list(zip(via[h], split_engines(topo.engines(h, cores[via[h][0]]), len(via[h])))) for h in helpers}
+    second = {h: list(zip(via[h], split_engines(topo.engines(h, cores[via[h][0]]), len(via[h])))) for h in hs}
     return first, straight, second
-
-
-def z_engines(cores, r, q, topo):
-    hs = helpers_of(cores, r, topo)
-    return topo.engines(cores[r], hs[q][0] if q in hs else cores[q])
 
 
 def helper_program(g, core, T, topo, r):
     cores = T.cores
-    hs = helpers_of(cores, r, topo)
     first, straight, second = ps_plan(cores, r, topo)
     sent = 0
     g.wait_ge(T.sem.psarr, sum(len(f[1]) for f in first if f[0] == core))
@@ -115,11 +117,11 @@ def helper_program(g, core, T, topo, r):
                                      src=T.ps32[:, PC * q:PC * (q + 1)], dst=T.psl[:, PC * (r ^ q):PC * ((r ^ q) + 1)]))
         sent += len(e)
     g.remote_dma_fused(trs, local_sem=T.sem.sent)
-    for q in sorted([q for q in hs if hs[q][0] == core], key=lambda q: hs[q][1]):
-        k = hs[q][1]
-        g.wait_ge(T.sem["arr%d" % k], len(z_engines(cores, r, q, topo)))
+    mine = [(t[3], q, t) for q, ts in block_plan(cores, r, topo).items() for t in ts if t[2] == core]
+    for k, q, (a, n, c, k, e) in sorted(mine):
+        g.wait_ge(T.sem["arr%d" % k], len(e))
         rid, pid = topo.addr(cores[q], core)
-        g.remote_dma(T.land[:, U * r:U * (r + 1)], T.land[:, U * k:U * (k + 1)], T.sem["arr%d" % r], T.sem.sent,
+        g.remote_dma(T.land[:, U * r + a:U * r + a + n], T.land[:, U * k:U * k + n], T.sem["arr%d" % r], T.sem.sent,
                      pid, rid, topo.mask(core, cores[q]))
         sent += len(topo.engines(core, cores[q]))
     g.wait_ge(T.sem.sent, sent)
@@ -130,7 +132,7 @@ def rank_program(g, core, T, topo):
     rank = T.rank_of(core)
     if rank is None:
         for r in range(N):
-            if core in topo.cores_of(cores[r]) and core in [h for h, k in helpers_of(cores, r, topo).values()]:
+            if core in topo.cores_of(cores[r]) and core in ps_plan(cores, r, topo)[2]:
                 helper_program(g, core, T, topo, r)
         return
     queue = {"v": g.vector, "s": g.scalar, "p": g.tensor, "g": g, "y": g.sync}
@@ -182,46 +184,62 @@ def rank_program(g, core, T, topo):
         return acc[:, 512 * b + a:512 * b + a + n]
     def copy(q, o, i, rd, wr):
         op(q, [(lambda: A.activation(o, i, ACT.Copy)) if q == "s" else (lambda: V.tensor_copy(o, i))], rd, wr)
+    def mult(o, a, b, rd, wr):
+        op("v", [lambda: V.tensor_tensor(o, a, b, ALU.mult)], rd, wr)
+    def scalar(o, i, x, f, rd, wr):
+        op("v", [lambda: V.tensor_scalar(o, i, x, None, f)], rd, wr)
+    def matmul(o, l, r, rd, wr):
+        op("p", [lambda: P.matmul(o, l, r, True, True)], rd, wr)
 
-    blocks = block_order(cores, rank, topo)
-    hs = helpers_of(cores, rank, topo)
+    direct, handed = peers(cores, rank, topo)
+    role = {"e1": rank, "e2": direct[0], "e3": direct[1], "e4": direct[2],
+            "r1": handed[0], "r2": handed[1], "r3": handed[2], "r4": handed[3]}
 
     total["psarr"] = 0
     for r in range(N):
         if r != rank:
-            h = helpers_of(cores, r, topo)
-            src = h[rank][0] if rank in h else cores[r]
-            total["arr%d" % r] = len(topo.engines(src, core))
+            total["arr%d" % r] = sum(len(t[4]) if t[2] == core else len(topo.engines(t[2], core))
+                                     for t in block_plan(cores, r, topo)[rank])
             wrote["land%d" % r] = ("arr%d" % r, total["arr%d" % r])
             first, straight, second = ps_plan(cores, r, topo)
             total["psarr"] += sum(len(e) for q, e in straight if q == rank)
             total["psarr"] += sum(len(e) for c in second for q, e in second[c] if q == rank)
     wrote["psl"] = ("psarr", total["psarr"])
 
-    sides = {"rep": (T.rep32[:], T.rep[:]), "mp": (T.mpc[:], T.mp[:]), "tr": (T.trz[:, 0:64], T.tr[:]),
-             "uc": (T.uc32[:], T.uc[:]), "ps": (T.ps32[:], T.ps[:])}
+    def load(q, name, o, i):
+        queue[q].dma_start(o, i).then_inc(T.sem["d_" + name], 16)
+        total["d_" + name] = 16
+        wrote["d_" + name] = ("d_" + name, 16)
+    load("s", "tr", T.trz[:, 0:64], T.tr[:])
+
+    f0, f1, fn, fg = OPT["fill"]
+    op("g", [lambda: g.iota(T.ia[:], [[0, 4], [-16, 8]], 128, 1)], [], ["ia"])
+    op("g", [lambda: g.iota(T.ib[:], [[16, 4], [-16, 8]], -64, 1)], [], ["ib"])
+    op("g", [lambda: g.iota(T.mw[:, S - fg:S], [[0, fg]], 0, 0)], [], ["mwg"])
+    op("g", [lambda: g.iota(T.ie[:], [[-8, 2], [-16, 9], [-256, 16]], 256 * 15, 1)], [], ["ie"])
+    op("g", [lambda: g.iota(T.ic[:], [[-16, 9], [-256, 4]], 128 + 256 * 3, 1)], [], ["ic"])
+    op("g", [lambda: g.iota(T.ii[:], [[-1, 128]], 0, 1)], [], ["ii"])
+    op("v", [lambda: V.memset(T.mw[:, 0:f0], 0)], [], ["mw0"])
+    op("v", [lambda: V.memset(T.trz[:, 64:80], 0.0)], [], ["trz"])
+    scalar(T.ia2[:], T.ia[:], 4, ALU.arith_shift_right, ["ia"], ["ia2"])
+    op("v", [lambda: V.memset(T.mw[:, f0:f0 + f1 // 3], 0)], [], ["mw1"])
+    scalar(T.gm[:], T.ia2[:], 8.0, ALU.is_equal, ["ia2"], ["gm"])
+    op("v", [lambda: V.memset(T.mw[:, f0 + f1 // 3:f0 + 2 * (f1 // 3)], 0)], [], ["mw1"])
+    mult(T.bt[:], T.ib[:], T.gm[:], ["ib", "gm"], ["bt"])
+    op("v", [lambda: V.memset(T.mw[:, f0 + 2 * (f1 // 3):f0 + f1], 0)], [], ["mw1"])
+    scalar(T.bdo[:], T.bt[:], 64.0, ALU.add, ["bt"], ["bdo"])
+    for k in range(fn):
+        a = f0 + f1 + f0 * k
+        copy("s", T.mw[:, a:a + f0], T.mw[:, 0:f0], ["mw0"], ["mws"])
+
+    sides = {"rep": (T.rep32[:], T.rep[:]), "mp": (T.mw[0:128:8, :], T.mp[:]), "uc": (T.uc32[:], T.uc[:]),
+             "ps": (T.ps32[:], T.ps[:])}
     for j in range(4):
         sides["x%d" % j] = (T.xs[:, 1024 * j:1024 * (j + 1)], T.x[:, 1024 * j:1024 * (j + 1)])
     for name in OPT["loads"].split():
-        queue["s" if name in OPT["on_s"] else "y"].dma_start(*sides[name]).then_inc(T.sem["d_" + name], 16)
-        total["d_" + name] = 16
-        wrote["d_" + name] = ("d_" + name, 16)
-
-    op("g", [lambda: g.iota(T.ie[:], [[-1, 8]], 8, 1)], [], ["ie"])
-    op("g", [lambda: g.iota(T.ia[:, 0:32], [[0, 4], [-16, 8]], 128, 1)], [], ["ia0"])
-    op("g", [lambda: g.iota(T.ib[:], [[16, 4], [-16, 8]], -64, 1)], [], ["ib"])
-    op("g", [lambda: g.iota(T.ia[:, 32:48], [[-16, 2], [-32, 8]], 128, 2)], [], ["ia1"])
-    op("g", [lambda: g.iota(T.ii[:], [[-1, 128]], 0, 1)], [], ["ii"])
-    op("v", [lambda: V.memset(T.trz[:, 64:80], 0.0)], [], ["trz"])
-    op("v", [lambda: V.tensor_scalar(T.ie2[:], T.ie[:], 7, None, ALU.bitwise_and)], ["ie"], ["ie2"])
-    op("v", [lambda: V.tensor_scalar(T.ia2[:], T.ia[:], 4, None, ALU.arith_shift_right)], ["ia0", "ia1"], ["ia2"])
-    op("v", [lambda: V.tensor_scalar(T.seg[:], T.ie2[:], 0.0, None, ALU.is_equal)], ["ie2"], ["seg"])
-    op("v", [lambda: V.tensor_scalar(T.gm[:], T.ia2[:, 0:32], 8.0, None, ALU.is_equal)], ["ia2"], ["gm"])
-    op("v", [lambda: V.tensor_scalar(T.sel[:], T.ia2[:, 32:48], 8.0, None, ALU.is_equal)], ["ia2"], ["sel"])
-    op("v", [lambda: V.tensor_tensor(T.bt[:], T.ib[:], T.gm[:], ALU.mult)], ["ib", "gm"], ["bt"])
-    op("v", [lambda: V.tensor_scalar(T.i16[:], T.ii[:], 0.0, None, ALU.is_equal)], ["ii"], ["i16"])
-    op("v", [lambda: V.tensor_scalar(T.bdo[:], T.bt[:], 64.0, None, ALU.add)], ["bt"], ["bdo"])
-    op("v", [lambda: V.tensor_scalar(T.i32[:], T.ii[:], 0.0, None, ALU.is_equal)], ["ii"], ["i32"])
+        if name == "mp":
+            order("y", [], ["mw0", "mw1", "mws", "mwg"])
+        load("y", name, *sides[name])
 
     order("g", ["d_ps"], [])
     total["sent"] = 0
@@ -236,182 +254,159 @@ def rank_program(g, core, T, topo):
             total["sent"] += len(e)
         g.remote_dma_fused(trs, local_sem=T.sem.sent)
 
-    op("v", [lambda: V.tensor_scalar(T.rhl[:, 0:128], T.rep32[:], 9, None, ALU.arith_shift_right)], ["d_rep"], ["rh"])
-    op("v", [lambda: V.tensor_scalar(T.rhl[:, 128:256], T.rep32[:], 511, None, ALU.bitwise_and)], ["d_rep"], ["rl"])
-    copy("v", T.ru16[:, 0:128], T.rhl[:, 0:128], ["rh"], ["rh16"])
-    copy("v", T.ru16[:, 128:256], T.rhl[:, 128:256], ["rl"], ["rl16"])
-    cuts, passes = OPT["cuts"], OPT["passes"]
-    G1 = ["g1_%d" % i for i in range(len(cuts) - 1)]
-    def mask_op(i):
-        a, b = cuts[i], cuts[i + 1]
-        copy("s", T.msk[:, a:b], T.seg[:, 0:8].indirect(T.ru16[:, a // 16:b // 16]), ["seg", "rh16"], ["msk%d" % i])
-    def g1_op(i):
-        a, b = cuts[i], cuts[i + 1]
-        op("v", [lambda: V.tensor_tensor(T.g1[:, a:b], T.mpc[:, 0:512].indirect(T.ru16[:, 128 + a // 16:128 + b // 16]),
-                                         T.msk[:, a:b], ALU.mult)], ["d_mp", "rl16", "msk%d" % i], ["g1_%d" % i])
+    def lookup(q, i):
+        copy(q, T.g1[:, 1024 * i:1024 * (i + 1)], T.mw[:].indirect(T.r16[:, 64 * i:64 * (i + 1)]), ["d_mp", "r16"], ["g1_%d" % i])
+    def slot_lookup(q, i):
+        b = 2 * (i ^ (rank // 4 * 2))
+        copy(q, T.g2[:, U * b:U * (b + 2)], T.g1[:].indirect(T.uc16[:, UC * b:UC * (b + 2)]), ["g1_0", "g1_1", "uc16"], ["g2_%d" % i])
+    def turn(i):
+        k, v = (i // 2) ^ (rank // 4), i % 2
+        op("p", [lambda j=j: P.matmul(bank(6 + v, 0, 4 * UC), T.sel[:, 144 * v + 15 - j:144 * v + 143 - j],
+                                      T.g2[:, 4 * U * k + j:4 * U * (k + 1):16], j == 0, j == 15) for j in range(16)],
+           ["sel", "g2_%d" % (i - v), "g2_%d" % (i - v + 1)], ["B%d" % (6 + v)])
+    def list_copy(q, i):
+        k, v = (i // 2) ^ (rank // 4), i % 2
+        a = N * UC * v + 4 * UC * k
+        copy(q, T.l16[:, a:a + 4 * UC], bank(6 + v, 0, 4 * UC), ["B%d" % (6 + v)], ["l16_%d_%d" % (k, v)])
 
-    pxb = [0, 2, 6, 0]
     def px_mm(j):
-        v, b = j // 2, pxb[j]
-        op("p", [lambda k=k: P.matmul(bank(b + k), T.bdb[:, 128 * v:128 * (v + 1)],
-                                      T.xs[:, 1024 * j + 512 * k:1024 * j + 512 * (k + 1)], True, True) for k in range(2)],
-           ["bdb", "d_x%d" % j], ["B%d" % b, "B%d" % (b + 1)])
-    def px_copy(q, j, h=None):
-        b = pxb[j]
-        if h is None:
-            copy(q, T.px[:, 1024 * j:1024 * (j + 1)], bank(b, 0, 1024), ["B%d" % b, "B%d" % (b + 1)], ["px%d0" % j, "px%d1" % j])
-        else:
-            copy(q, T.px[:, 1024 * j + 512 * h:1024 * j + 512 * (h + 1)], bank(b + h), ["B%d" % (b + h)], ["px%d%d" % (j, h)])
+        matmul(bank(j % 6), T.bdb[:, 128 * (j // 4):128 * (j // 4 + 1)], T.xs[:, 512 * j:512 * (j + 1)],
+               ["bdb", "d_x%d" % (j // 2)], ["B%d" % (j % 6)])
+    def px_copy(q, j):
+        copy(q, T.px[:, 512 * j:512 * (j + 1)], bank(j % 6), ["B%d" % (j % 6)], ["px%d" % j])
 
-    def g2_op(k):
-        q = blocks[k]
-        copy("v", T.g2[:, U * k:U * (k + 1)], T.g1[:, 0:C].indirect(T.uc16[:, UC * q:UC * (q + 1)]), G1 + ["uc16"], ["g2_%d" % k])
-    def span(i):
-        return passes[i], passes[i + 1], UC * (passes[i + 1] - passes[i])
-    def turn1(i):
-        k0, k1, n = span(i)
-        op("p", [lambda b=b: P.matmul(acc[0:n, 2048 + b:2048 + 256:16], T.g2[:, U * k0 + b:U * k1:16], T.sel[:], True, True)
-                 for b in range(16)], ["sel"] + ["g2_%d" % k for k in range(k0, k1)], ["B4"])
-    def turn1_copy(i):
-        k0, k1, n = span(i)
-        copy("v", T.t1[0:n, 256 * i:256 * (i + 1)], acc[0:n, 2048:2048 + 256], ["B4"], ["t1_%d" % i])
-    def turn2(i):
-        k0, k1, n = span(i)
-        op("p", [lambda v=v: P.matmul(bank(5, n * v, n), T.t1[0:n, 256 * i + 128 * v:256 * i + 128 * (v + 1)],
-                                      T.i16[0:n, 0:n], True, True) for v in range(2)], ["t1_%d" % i, "i16"], ["B5"])
-    def turn2_copy(i):
-        k0, k1, n = span(i)
-        copy("v", T.l16[:, 2 * UC * k0:2 * UC * k1], bank(5, 0, 2 * n), ["B5"], ["l16_%d" % i])
-    def lists(k, v):
-        i = [j for j in range(len(passes) - 1) if passes[j] <= k < passes[j + 1]][0]
-        k0, k1, n = span(i)
-        a = 2 * UC * k0 + n * v + UC * (k - k0)
-        return T.l16[:, a:a + UC], "l16_%d" % i
+    zb = {role[c]: b for c, b in (("r1", 0), ("r2", 1), ("e2", 2), ("r3", 3), ("r4", 0), ("e4", 1))}
+    p2 = T.raw[:, 0:128]
+    def blk(buf, q):
+        return buf[:, U * q:U * (q + 1)]
+    def send(q, name):
+        order("g", [name], [])
+        trs = []
+        for a, n, c, k, es in block_plan(cores, rank, topo)[q]:
+            rid, pid = topo.addr(c, core)
+            src, dst = (T.raw[:], T.lraw[:]) if q == role["e3"] else (T.zs[:, U * q + a:U * q + a + n], T.land[:, U * k:U * k + n])
+            trs.append(RemoteDMATransfer(dst_ids=[DstId(rid=rid, pnc=pid)], dma_engine_mask=bits(es), remote_sem=T.sem["arr%d" % k],
+                                         src=src, dst=dst))
+            total["sent"] += len(es)
+        g.remote_dma_fused(trs, local_sem=T.sem.sent)
+    def a_op(e, q):
+        copy(e, blk(T.ab, q), T.px[:, 0:C].indirect(T.l16[:, UC * q:UC * (q + 1)]),
+             ["l16_%d_0" % (q // 4), "px0", "px1", "px2", "px3"], ["ab%d" % q])
+    def b_op(q):
+        out = blk(T.land, q) if q == rank else T.raw[:, 128:] if q == role["e3"] else blk(T.x2, q)
+        name = ("land%d" if q == rank else "x2_%d") % q
+        mult(out, T.px[:, C:2 * C].indirect(T.l16[:, UC * (N + q):UC * (N + q + 1)]), blk(T.ab, q),
+             ["l16_%d_1" % (q // 4), "px4", "px5", "px6", "px7", "ab%d" % q], [name])
+        if q in zb:
+            matmul(bank(zb[q], 0, U), p2, out, ["p2", name], ["B%d" % zb[q]])
+        elif q != rank:
+            order("g", ["p2"], [])
+            send(q, name)
+    def z_op(e, q):
+        copy(e, blk(T.zs, q), bank(zb[q], 0, U), ["B%d" % zb[q]], ["zs%d" % q])
+        send(q, "zs%d" % q)
 
-    zbank = [6, 7, 2, 3]
-    def a_op(k):
-        ap, t = lists(k, 0)
-        copy("s", T.ab[:, U * k:U * (k + 1)], T.px[:, 0:C].indirect(ap), [t, "px00", "px01", "px10", "px11"], ["ab%d" % k])
-    def x2_op(k):
-        ap, t = lists(k, 1)
-        op("v", [lambda: V.tensor_tensor(T.x2[:, U * k:U * (k + 1)], T.px[:, C:2 * C].indirect(ap), T.ab[:, U * k:U * (k + 1)],
-                                         ALU.mult)], [t, "px20", "px21", "px30", "px31", "ab%d" % k], ["x2_%d" % k])
-        b = zbank[k % 4]
-        op("p", [lambda: P.matmul(bank(b, 0, U), T.bdf[:, 0:128], T.x2[:, U * k:U * (k + 1)], True, True)],
-           ["bdf", "x2_%d" % k], ["B%d" % b])
-    def z_op(eng, k):
-        q = blocks[k]
-        b = zbank[k % 4]
-        o = T.land[:, U * q:U * (q + 1)] if q == rank else T.zs[:, U * k:U * (k + 1)]
-        copy(eng, o, bank(b, 0, U), ["B%d" % b], ["land%d" % q if q == rank else "zs%d" % k])
-        if q == rank:
-            return
-        order("g", ["zs%d" % k], [])
-        dst, slot = hs[q] if q in hs else (cores[q], rank)
-        rid, pid = topo.addr(dst, core)
-        e = z_engines(cores, rank, q, topo)
-        g.remote_dma(T.land[:, U * slot:U * (slot + 1)], o, T.sem["arr%d" % slot], T.sem.sent, pid, rid, bits(e))
-        total["sent"] += len(e)
-
-    def due(r):
-        if r == rank:
-            return OPT["own_due"]
-        return block_order(cores, r, topo).index(rank) + (OPT["relay_lag"] if rank in helpers_of(cores, r, topo) else 0)
-    def win(r):
-        return T.land[:, U * r:U * (r + 1)].indirect(T.po16[:, PC * (r ^ rank):PC * ((r ^ rank) + 1)])
-    def po(r):
-        return "po_own" if r == rank else "po16"
+    top = {role["e1"]: 4, role["e3"]: 0}
+    wbank = {"1e": 5, "1a": 2, "1b": 3, "2e": 1, "2a": 5, "2b": 2}
     def xe(r):
         return T.xe[:, TT * r:TT * (r + 1)]
-    def expand(r):
-        copy("s", xe(r), win(r), ["land%d" % r, po(r)], ["xe%d" % r])
-    def to_psum(r, b):
-        copy("s", bank(b), xe(r), ["xe%d" % r], ["B%d" % b])
-    def kt(y):
-        return 3 * (y // 4) + y % 4 - 1
-    def col(buf, y, a=0, n=TT):
-        return buf[:, TT * kt(y) + a:TT * kt(y) + a + n]
-    wb = {}
-    def w_mm(y, b):
-        wb[y] = b
-        op("p", [lambda: P.matmul(bank(b), T.bdf[:, 128:256], col(T.ll, y), True, True)], ["bdf", "l%d" % y], ["B%d" % b])
-    def l_gather(y, a, b, w):
-        op("v", [lambda: V.tensor_tensor(col(T.ll, y), win(a), xe(b), ALU.mult)], ["land%d" % a, po(a), "xe%d" % b], ["l%d" % y])
-        w_mm(y, w)
-    def l_psum(y, a, b, w):
-        op("v", [lambda: V.tensor_tensor(col(T.ll, y), xe(a), bank(b), ALU.mult)], ["xe%d" % a, "B%d" % b], ["l%d" % y])
-        w_mm(y, w)
-    def u_op(y, a=0, n=TT):
-        b = wb[y]
-        op("v", [lambda: V.tensor_tensor(bank(b, a, n), xe(y)[:, a:a + n], bank(b, a, n), ALU.mult)],
-           ["xe%d" % y, "B%d" % b], ["B%d" % b])
-    def v_op(y, a=0, n=TT):
-        b = wb[y]
-        src, tok = (T.hh, "hh") if y == role["x3"] and "h" in OPT["sched"] else (xe(4 * (y // 4)), "xe%d" % (4 * (y // 4)))
-        op("v", [lambda: V.tensor_tensor(col(T.vv, y, a, n), src[:, a:a + n], bank(b, a, n), ALU.mult)],
-           [tok, "B%d" % b], ["v%d_%d" % (y, h) for h in range(a // 128, (a + n) // 128)])
-    def rcol(c):
-        return 512 * (5 + c // 2) + 48 * (c % 2)
-    def r_mm(y, a=0, n=TT):
-        for c in range(a // 128, (a + n) // 128):
-            op("p", [lambda: P.matmul(acc[:, rcol(c) + kt(y):rcol(c) + 48:6], col(T.vv, y, 128 * c, 128), T.gm[:, 0:8], True, True)],
-               ["gm", "v%d_%d" % (y, c)], ["B%d" % (5 + c // 2)])
-    def r_copy(q, c, n):
-        copy(q, T.rs[:, 48 * c:48 * (c + n)], acc[:, rcol(c):rcol(c) + 48 * n], ["B%d" % (5 + c // 2)],
-             ["rs%d" % k for k in range(c, c + n)])
-    tb = OPT["tb"]
-    def tcol(c):
-        return 512 * tb[c] + 128 * c
-    def t_mm(c):
-        op("p", [lambda: P.transpose(acc[0:48, tcol(c):tcol(c) + 128], T.rs[:, 48 * c:48 * (c + 1)], T.i32[:])],
-           ["rs%d" % c, "i32"], ["B%d" % tb[c]])
-    def y_copy(q, c, n):
-        copy(q, T.ys[0:48, 128 * c:128 * (c + n)], acc[0:48, tcol(c):tcol(c) + 128 * n], ["B%d" % tb[c]],
-             ["ys%d" % k for k in range(c, c + n)])
+    def expand(e, r):
+        win = T.lraw[:, 128:] if r == role["e3"] else blk(T.land, r)
+        copy(e, xe(r), win.indirect(T.po16[:, PC * (r ^ rank):PC * ((r ^ rank) + 1)]),
+             ["land%d" % r, "po_own" if r == rank else "po16"], ["xe%d" % r])
+        if r in top:
+            matmul(bank(top[r]), p2 if r == rank else T.lraw[:, 0:128], xe(r), ["p2", "land%d" % r, "xe%d" % r], ["B%d" % top[r]])
+    def join(name):
+        x, e, a, b = [role[c] for c in ("e1 e2 r1 r2" if name[0] == "1" else "e3 e4 r3 r4").split()]
+        y, c, d = {"e": (e, a, b), "a": (a, e, b), "b": (b, e, a)}[name[1]]
+        h = (x, y) if 0 in (x % 4, y % 4) else (c, d)
+        return 3 * (x // 4) + max(h[0] % 4, h[1] % 4) - 1, x, y, c, d
+    def col(buf, j, a=0, n=TT):
+        return buf[:, TT * j + a:TT * j + a + n]
+    def m_step(name):
+        j, x, y, c, d = join(name)
+        mult(col(T.ll, j), xe(y), bank(top[x]), ["xe%d" % y, "B%d" % top[x]], ["l%d" % j])
+        k = 1 if 0 in (x % 4, y % 4) else 0
+        matmul(bank(wbank[name]), T.bdw[:, 128 * k:128 * (k + 1)], col(T.ll, j), ["w", "wt", "l%d" % j], ["B%d" % wbank[name]])
+    def u_step(name):
+        j, x, y, c, d = join(name)
+        b = wbank[name]
+        mult(bank(b), xe(c), bank(b), ["xe%d" % c, "B%d" % b], ["B%d" % b])
+    def v_op(name, a=0, n=TT):
+        j, x, y, c, d = join(name)
+        b = wbank[name]
+        mult(col(T.vv, j, a, n), xe(d)[:, a:a + n], bank(b, a, n), ["xe%d" % d, "B%d" % b],
+             ["v%d_%d" % (j, i) for i in range(a // 128, (a + n) // 128)])
+        return j
+    summed = {"1": ["1e", "1a", "1b"], "2": ["2e", "2a"]}
+    def v_step(name):
+        j = v_op(name)
+        i = (summed["1"] + summed["2"]).index(name)
+        op("p", [lambda c=c: P.matmul(acc[:, 512 * 6 + 32 * i + c:512 * 6 + 32 * (i + 1):4], col(T.vv, j, 128 * c, 128),
+                                      T.ones[:, 3:35:4], True, True) for c in range(4)],
+           ["ones"] + ["v%d_%d" % (j, c) for c in range(4)], ["B6", "sum" + name])
+    total["ydone"] = 0
+    def store(j, p, a, name):
+        order("y", [name], [])
+        g.sync.dma_start(T.y[:, TT * j:TT * (j + 1)], T.ys[p:p + 32, a:a + 128]).then_inc(T.sem.ydone, 16)
+        total["ydone"] += 16
+    def turn_sums(e, k):
+        n, a = 32 * len(summed[k]), int(k) - 1
+        copy(e, T.rs[:, 96 * a:96 * a + n], bank(6, 96 * a, n), ["B6"] + ["sum" + j for j in summed[k]], ["rs" + k])
+        op("p", [lambda: P.transpose(acc[0:n, 512 * 7:512 * 7 + 128], T.rs[:, 96 * a:96 * a + n], T.i32[:])],
+           ["rs" + k, "i32"], ["B7"])
+    def store_sums(e, k):
+        n, a = 32 * len(summed[k]), int(k) - 1
+        copy(e, T.ys[0:n, 128 * a:128 * (a + 1)], acc[0:n, 512 * 7:512 * 7 + 128], ["B7"], ["ys" + k])
+        for i, name in enumerate(summed[k]):
+            store(join(name)[0], 32 * i, 128 * a, "ys" + k)
+    def last():
+        for a, n in ((0, 2), (2, 1), (3, 1)):
+            j = v_op("2b", 128 * a, 128 * n)
+            op("p", [lambda c=c: P.matmul(acc[0:32, 2048:2176], T.ones[:, 3 - c:35 - c], col(T.vv, j, 128 * c, 128), c == 0, c == 3)
+                     for c in range(a, a + n)], ["ones"] + ["v%d_%d" % (j, c) for c in range(a, a + n)], ["B4"])
+        copy("s", T.ys[0:32, 256:384], acc[0:32, 2048:2176], ["B4"], ["ys3"])
+        store(j, 0, 256, "ys3")
+    def constants():
+        scalar(T.ic2[:], T.ic[:], 4, ALU.arith_shift_right, ["ic"], ["ic2"])
+        scalar(T.i32[:], T.ii[:], 0.0, ALU.is_equal, ["ii"], ["i32"])
+        scalar(T.ones[:], T.ic2[:], 8.0, ALU.is_equal, ["ic2"], ["ones"])
+    def diag(q, out, a, n, name):
+        copy(q, out, T.trz[:, 0:80].indirect(T.bdo[:, a:a + n]), ["d_tr", "trz", "bdo"], [name])
+    def w_turned(e):
+        matmul(bank(7, 0, 128), T.bdw[:, 0:128], T.i32[:], ["w", "i32"], ["B7"])
+        copy(e, T.bdw[:, 128:256], bank(7, 0, 128), ["B7"], ["wt"])
 
-    a1 = 4 * (rank // 4)
-    a2 = 4 - a1
-    x1, x2, x3 = sorted(range(a1 + 1, a1 + 4), key=due)
-    z1, z2, z3 = sorted(range(a2 + 1, a2 + 4), key=due)
-    role = {"a1": a1, "a2": a2, "x1": x1, "x2": x2, "x3": x3, "z1": z1, "z2": z2, "z3": z3}
-    def diag(q, out, a, name):
-        copy(q, out, T.trz[:, 0:80].indirect(T.bdo[:, a:a + 16]), ["d_tr", "trz", "bdo"], [name])
-    step = {
-        "bdb": lambda: diag("s", T.bdb[:], 0, "bdb"), "bdf": lambda: diag("s", T.bdf[:], 16, "bdf"),
-        "bvb": lambda: diag("v", T.bdb[:], 0, "bdb"), "bvf": lambda: diag("v", T.bdf[:], 16, "bdf"),
-        "uc": lambda: copy("v", T.uc16[:], T.uc32[:], ["d_uc"], ["uc16"]),
-        "po": lambda: copy("v", T.po16[:, PC:], T.psl[:, PC:], ["psl"], ["po16"]),
-        "pown": lambda: copy("v", T.po16[:, 0:PC], T.ps32[:, PC * rank:PC * (rank + 1)], ["d_ps"], ["po_own"]),
-        "h": lambda: op("v", [lambda: V.tensor_tensor(T.hh[:], win(x3), xe(a1), ALU.mult)],
-                        ["land%d" % x3, po(x3), "xe%d" % a1], ["hh"]),
-        "lg3": lambda: l_gather(x3, x2, x1, 2), "lg2": lambda: l_gather(x2, x3, x1, 3), "lg1": lambda: l_gather(x1, x3, x2, 4),
-        "p1": lambda: to_psum(z1, 7), "p2": lambda: to_psum(z2, 1),
-        "lp3": lambda: l_psum(z3, z2, 7, 2), "lp2": lambda: l_psum(z2, z3, 7, 3), "lp1": lambda: l_psum(z1, z3, 1, 4),
+    step = {"bdb": lambda: diag("s", T.bdb[:], 0, 16, "bdb"), "cst": constants, "end": last,
+            "sel": lambda: scalar(T.sel[:], T.ie[:], 0.0, ALU.is_equal, ["ie"], ["sel"])}
+    by_queue = {
+        "p2": lambda e: diag(e, p2, 16, 8, "p2"), "w": lambda e: diag(e, T.bdw[:, 0:128], 24, 8, "w"), "wt": w_turned,
+        "r": lambda e: copy(e, T.r16[:], T.rep32[:], ["d_rep"], ["r16"]),
+        "uc": lambda e: copy(e, T.uc16[:], T.uc32[:], ["d_uc"], ["uc16"]),
+        "po": lambda e: copy(e, T.po16[:, PC:], T.psl[:, PC:], ["psl"], ["po16"]),
+        "o": lambda e: copy(e, T.po16[:, 0:PC], T.ps32[:, PC * rank:PC * (rank + 1)], ["d_ps"], ["po_own"]),
     }
-    by_number = {"m": mask_op, "g": g1_op, "G": g2_op, "pm": px_mm, "ta": turn1, "tb": turn1_copy, "tc": turn2, "td": turn2_copy,
-                 "a": a_op, "x": x2_op, "zs": lambda k: z_op("s", k), "zv": lambda k: z_op("v", k),
-                 "pcs": lambda j: px_copy("s", j), "pcv": lambda j: px_copy("v", j),
-                 "phs": lambda j: px_copy("s", j // 2, j % 2), "phv": lambda j: px_copy("v", j // 2, j % 2)}
-    by_role = {"e": expand, "u": u_op, "v": v_op, "r": r_mm}
-    for s in OPT["sched"] + OPT["tail"].split():
+    by_number = {"p": px_copy, "g": lookup, "G": slot_lookup, "l": list_copy}
+    by_name = {"a": a_op, "z": z_op, "x": expand, "f": turn_sums, "y": store_sums}
+    alone = {"b": b_op, "m": m_step, "u": u_step, "v": v_step}
+    for s in OPT["sched"]:
+        f, dot, w = s.partition(".")
         if s in step:
             step[s]()
-        elif s.count(".") == 3:
-            f, y, a, n = s.split(".")
-            by_role[f](role[y], 128 * int(a), 128 * int(n))
-        elif "." in s:
-            by_role[s.split(".")[0]](role[s.split(".")[1]])
-        elif s[0] in "RY":
-            (r_copy if s[0] == "R" else y_copy)(s[1], int(s[2]), int(s[3]))
-        elif s[0] == "T":
-            t_mm(int(s[1]))
+        elif dot and f in alone:
+            alone[f](role.get(w, w))
+        elif dot:
+            by_name[f[0]](f[1], role.get(w, w))
+        elif s[:-1] in by_queue:
+            by_queue[s[:-1]](s[-1])
+        elif s[:-1] == "pm":
+            px_mm(int(s[-1]))
+        elif s[0] == "t":
+            turn(int(s[1]))
         else:
-            by_number[s[:-1]](int(s[-1]))
+            by_number[s[0]](s[1], int(s[2]))
 
-    order("y", ["ys0", "ys1", "ys2", "ys3"], [])
-    g.sync.dma_start(T.y[:], T.ys[0:48, :]).then_inc(T.sem.ydone, 16)
-    total["ydone"] = 16
     for s in total:
         if s != "ydone" and max(waited[q].get(s, 0) for q in waited) < total[s]:
             wait("g", s, total[s])
-    wait("y", "ydone", 16)
+    wait("y", "ydone", total["ydone"])

from concourse.bass import DstId, RemoteDMATransfer
from concourse.mybir import AluOpType as ALU, ActivationFunctionType as ACT

N, C, S, TT, U = 8, 2048, 4096, 512, 320
UC = U // 16
PC = TT // 16


def _sb(n, d):
    return ("sbuf", [128, n], d)


SCRATCH = {
    "xs": _sb(2 * C, "bfloat16"), "trz": _sb(80, "bfloat16"), "mw": _sb(S, "int32"), "rep32": _sb(128, "int32"),
    "r16": _sb(128, "uint16"), "uc32": _sb(N * UC, "int32"), "uc16": _sb(N * UC, "uint16"),
    "ps32": _sb(N * PC, "int32"), "psl": _sb(N * PC, "int32"), "po16": _sb(N * PC, "uint16"),
    "ia": _sb(32, "int32"), "ia2": _sb(32, "int32"), "ib": _sb(32, "int32"), "ic": _sb(36, "int32"), "ic2": _sb(36, "int32"),
    "ie": _sb(288, "int32"), "ii": _sb(128, "int32"), "gm": _sb(32, "float32"), "bt": _sb(32, "float32"),
    "bdo": _sb(32, "uint16"), "ones": _sb(36, "float32"), "sel": _sb(288, "float16"), "i32": _sb(128, "float32"),
    "bdb": _sb(256, "bfloat16"), "bdw": _sb(256, "float32"), "g1": _sb(C, "float32"), "g2": _sb(N * U, "float16"),
    "l16": _sb(2 * N * UC, "uint16"), "px": _sb(2 * C, "float32"), "ab": _sb(N * U, "float32"), "x2": _sb(N * U, "float32"),
    "zs": _sb(N * U, "float32"), "land": _sb(N * U, "float32"), "raw": _sb(128 + U, "float32"), "lraw": _sb(128 + U, "float32"),
    "xe": _sb(N * TT, "float32"), "ll": _sb(6 * TT, "float32"), "vv": _sb(6 * TT, "float32"),
    "rs": _sb(192, "float32"), "ys": _sb(384, "float32"), "acc": ("psum", [128, 4096], "float32"),
}
SEMAPHORES = (["cv", "cs", "cp", "cg", "sent", "psarr", "ydone"] + ["arr%d" % r for r in range(N)]
              + ["d_rep", "d_mp", "d_tr", "d_uc", "d_ps", "d_x0", "d_x1", "d_x2", "d_x3"])

OPT = {
    "fill": [384, 1536, 4, 640],
    "loads": "rep uc x0 mp x1 x2 x3 ps",
    "via": "f0n0 f1n1 F0 F1",
    "sched": """rv ucv bdb pm0 p2v cst ws pm1 pv0 pm3 pm2 ps1 gs1 pm5 sel pm4 gv0 Gs1 Gv0 pm6 pm7 pv4 ps3 t0 ps2 pv6 ls0
        t1 ps7 Gs2 pv5 Gs3 av.r1 lv1 b.r1 zs.r1 wts ov av.r2 t2 b.r2 av.e1 lv2 t3 as.e2 as.e3 zs.r2 ls3 b.e2 av.r3
        as.r4 b.r3 zs.e2 b.e1 b.r4 as.e4 zs.r3 b.e3 pos xs.e1 b.e4 zv.r4 xs.e2 xs.r2 xv.r1 m.1a m.1e m.1b u.1a u.1e
        zs.e4 xs.e3 xs.r3 xs.e4 v.1a u.1b v.1e v.1b m.2a m.2e u.2a fs.1 xs.r4 m.2b ys.1 u.2e v.2a v.2e u.2b fv.2 ys.2
        end""".split(),
}


def bits(engines):
    m = 0
    for e in engines:
        m |= 1 << e
    return m


def split_engines(engines, k):
    sizes = [1] * k
    while True:
        i = sizes.index(min(sizes))
        if sum(sizes) + sizes[i] > len(engines):
            break
        sizes[i] *= 2
    out, a = [], 0
    for s in sizes:
        out.append(engines[a:a + s])
        a += s
    return out


def peers(cores, r, topo):
    others = [r ^ m for m in range(1, N)]
    direct = [q for q in others if topo.may_write(cores[r], cores[q])]
    return direct, [q for q in others if q not in direct]


def helpers(cores, r, topo):
    me = cores[r]
    able = [c for c in topo.cores_of(me)
            if c not in cores and all(topo.may_write(c, cores[q]) for q in peers(cores, r, topo)[1])]
    return [c for c in able if topo.die(c) != topo.die(me)], [c for c in able if topo.die(c) == topo.die(me)]


def block_plan(cores, r, topo):
    me = cores[r]
    direct, handed = peers(cores, r, topo)
    far, near = helpers(cores, r, topo)
    plan = {q: [(0, U, cores[q], r, topo.engines(me, cores[q]))] for q in direct}
    seen = {}
    for q, w in zip(handed, OPT["via"].split()):
        hs = [(far if w[i] in "fF" else near)[int(w[i + 1])] for i in range(0, len(w), 2)]
        free = topo.engines(me, hs[0])
        if w[0].isupper():
            free = [e for e in free if e not in topo.engines(me, cores[direct[0]])]
        n = U // len(hs)
        plan[q] = []
        for i, (c, e) in enumerate(zip(hs, split_engines(free, len(hs)))):
            plan[q].append((n * i, n, c, seen.get(c, 0), e))
            seen[c] = seen.get(c, 0) + 1
    return plan


def ps_plan(cores, r, topo):
    me = cores[r]
    direct, handed = peers(cores, r, topo)
    hs = sorted(set(t[2] for ts in block_plan(cores, r, topo).values() for t in ts if t[2] not in cores))
    rel = sorted(handed)
    per = len(rel) // len(hs)
    via = {h: rel[per * i:per * (i + 1)] for i, h in enumerate(hs)}
    width = max(max(v) - min(v) + 1 for v in via.values())
    first = [(h, e, min(min(via[h]), N - width), width) for h, e in zip(hs, split_engines(topo.engines(me, hs[0]), len(hs)))]
    straight = list(zip(direct, split_engines(topo.engines(me, cores[direct[0]]), len(direct))))
    second = {h: list(zip(via[h], split_engines(topo.engines(h, cores[via[h][0]]), len(via[h])))) for h in hs}
    return first, straight, second


def helper_program(g, core, T, topo, r):
    cores = T.cores
    first, straight, second = ps_plan(cores, r, topo)
    sent = 0
    g.wait_ge(T.sem.psarr, sum(len(f[1]) for f in first if f[0] == core))
    trs = []
    for q, e in second[core]:
        rid, pid = topo.addr(cores[q], core)
        trs.append(RemoteDMATransfer(dst_ids=[DstId(rid=rid, pnc=pid)], dma_engine_mask=bits(e), remote_sem=T.sem.psarr,
                                     src=T.ps32[:, PC * q:PC * (q + 1)], dst=T.psl[:, PC * (r ^ q):PC * ((r ^ q) + 1)]))
        sent += len(e)
    g.remote_dma_fused(trs, local_sem=T.sem.sent)
    mine = [(t[3], q, t) for q, ts in block_plan(cores, r, topo).items() for t in ts if t[2] == core]
    for k, q, (a, n, c, k, e) in sorted(mine):
        g.wait_ge(T.sem["arr%d" % k], len(e))
        rid, pid = topo.addr(cores[q], core)
        g.remote_dma(T.land[:, U * r + a:U * r + a + n], T.land[:, U * k:U * k + n], T.sem["arr%d" % r], T.sem.sent,
                     pid, rid, topo.mask(core, cores[q]))
        sent += len(topo.engines(core, cores[q]))
    g.wait_ge(T.sem.sent, sent)


def rank_program(g, core, T, topo):
    cores = T.cores
    rank = T.rank_of(core)
    if rank is None:
        for r in range(N):
            if core in topo.cores_of(cores[r]) and core in ps_plan(cores, r, topo)[2]:
                helper_program(g, core, T, topo, r)
        return
    queue = {"v": g.vector, "s": g.scalar, "p": g.tensor, "g": g, "y": g.sync}
    esem = {"v": "cv", "s": "cs", "p": "cp", "g": "cg"}
    total = {}
    waited = {k: {} for k in queue}
    wrote, read = {}, {}

    def wait(q, sem, n):
        if waited[q].get(sem, 0) < n:
            queue[q].wait_ge(T.sem[sem], n)
            waited[q][sem] = n

    def order(q, rd, wr):
        mine = esem.get(q)
        need = {}
        def add(s, n):
            need[s] = max(need.get(s, 0), n)
        for t in rd:
            add(*wrote[t])
            if t[0] == "B":
                for s, n in read.get(t, {}).items():
                    if s != mine:
                        add(s, n)
        for t in wr:
            if t in wrote and wrote[t][0] != mine:
                add(*wrote[t])
            for s, n in read.get(t, {}).items():
                if s != mine:
                    add(s, n)
        for s in need:
            wait(q, s, need[s])

    def op(q, calls, rd, wr):
        order(q, rd, wr)
        s = esem[q]
        for c in calls:
            c().then_inc(T.sem[s], 1)
            total[s] = total.get(s, 0) + 1
        for t in rd:
            read.setdefault(t, {})[s] = total[s]
        for t in wr:
            wrote[t] = (s, total[s])
            read[t] = {}

    V, A, P = g.vector, g.scalar, g.tensor
    acc = T.acc
    def bank(b, a=0, n=512):
        return acc[:, 512 * b + a:512 * b + a + n]
    def copy(q, o, i, rd, wr):
        op(q, [(lambda: A.activation(o, i, ACT.Copy)) if q == "s" else (lambda: V.tensor_copy(o, i))], rd, wr)
    def mult(o, a, b, rd, wr):
        op("v", [lambda: V.tensor_tensor(o, a, b, ALU.mult)], rd, wr)
    def scalar(o, i, x, f, rd, wr):
        op("v", [lambda: V.tensor_scalar(o, i, x, None, f)], rd, wr)
    def matmul(o, l, r, rd, wr):
        op("p", [lambda: P.matmul(o, l, r, True, True)], rd, wr)

    direct, handed = peers(cores, rank, topo)
    role = {"e1": rank, "e2": direct[0], "e3": direct[1], "e4": direct[2],
            "r1": handed[0], "r2": handed[1], "r3": handed[2], "r4": handed[3]}

    total["psarr"] = 0
    for r in range(N):
        if r != rank:
            total["arr%d" % r] = sum(len(t[4]) if t[2] == core else len(topo.engines(t[2], core))
                                     for t in block_plan(cores, r, topo)[rank])
            wrote["land%d" % r] = ("arr%d" % r, total["arr%d" % r])
            first, straight, second = ps_plan(cores, r, topo)
            total["psarr"] += sum(len(e) for q, e in straight if q == rank)
            total["psarr"] += sum(len(e) for c in second for q, e in second[c] if q == rank)
    wrote["psl"] = ("psarr", total["psarr"])

    def load(q, name, o, i):
        queue[q].dma_start(o, i).then_inc(T.sem["d_" + name], 16)
        total["d_" + name] = 16
        wrote["d_" + name] = ("d_" + name, 16)
    load("s", "tr", T.trz[:, 0:64], T.tr[:])

    f0, f1, fn, fg = OPT["fill"]
    op("g", [lambda: g.iota(T.ia[:], [[0, 4], [-16, 8]], 128, 1)], [], ["ia"])
    op("g", [lambda: g.iota(T.ib[:], [[16, 4], [-16, 8]], -64, 1)], [], ["ib"])
    op("g", [lambda: g.iota(T.mw[:, S - fg:S], [[0, fg]], 0, 0)], [], ["mwg"])
    op("g", [lambda: g.iota(T.ie[:], [[-8, 2], [-16, 9], [-256, 16]], 256 * 15, 1)], [], ["ie"])
    op("g", [lambda: g.iota(T.ic[:], [[-16, 9], [-256, 4]], 128 + 256 * 3, 1)], [], ["ic"])
    op("g", [lambda: g.iota(T.ii[:], [[-1, 128]], 0, 1)], [], ["ii"])
    op("v", [lambda: V.memset(T.mw[:, 0:f0], 0)], [], ["mw0"])
    op("v", [lambda: V.memset(T.trz[:, 64:80], 0.0)], [], ["trz"])
    scalar(T.ia2[:], T.ia[:], 4, ALU.arith_shift_right, ["ia"], ["ia2"])
    op("v", [lambda: V.memset(T.mw[:, f0:f0 + f1 // 3], 0)], [], ["mw1"])
    scalar(T.gm[:], T.ia2[:], 8.0, ALU.is_equal, ["ia2"], ["gm"])
    op("v", [lambda: V.memset(T.mw[:, f0 + f1 // 3:f0 + 2 * (f1 // 3)], 0)], [], ["mw1"])
    mult(T.bt[:], T.ib[:], T.gm[:], ["ib", "gm"], ["bt"])
    op("v", [lambda: V.memset(T.mw[:, f0 + 2 * (f1 // 3):f0 + f1], 0)], [], ["mw1"])
    scalar(T.bdo[:], T.bt[:], 64.0, ALU.add, ["bt"], ["bdo"])
    for k in range(fn):
        a = f0 + f1 + f0 * k
        copy("s", T.mw[:, a:a + f0], T.mw[:, 0:f0], ["mw0"], ["mws"])

    sides = {"rep": (T.rep32[:], T.rep[:]), "mp": (T.mw[0:128:8, :], T.mp[:]), "uc": (T.uc32[:], T.uc[:]),
             "ps": (T.ps32[:], T.ps[:])}
    for j in range(4):
        sides["x%d" % j] = (T.xs[:, 1024 * j:1024 * (j + 1)], T.x[:, 1024 * j:1024 * (j + 1)])
    for name in OPT["loads"].split():
        if name == "mp":
            order("y", [], ["mw0", "mw1", "mws", "mwg"])
        load("y", name, *sides[name])

    order("g", ["d_ps"], [])
    total["sent"] = 0
    first, straight, second = ps_plan(cores, rank, topo)
    for plan in ([(c, e, q0, n, T.ps32, q0) for c, e, q0, n in first],
                 [(cores[q], e, q, 1, T.psl, q ^ rank) for q, e in straight]):
        trs = []
        for c, e, q0, n, to, k in plan:
            rid, pid = topo.addr(c, core)
            trs.append(RemoteDMATransfer(dst_ids=[DstId(rid=rid, pnc=pid)], dma_engine_mask=bits(e), remote_sem=T.sem.psarr,
                                         src=T.ps32[:, PC * q0:PC * (q0 + n)], dst=to[:, PC * k:PC * (k + n)]))
            total["sent"] += len(e)
        g.remote_dma_fused(trs, local_sem=T.sem.sent)

    def lookup(q, i):
        copy(q, T.g1[:, 1024 * i:1024 * (i + 1)], T.mw[:].indirect(T.r16[:, 64 * i:64 * (i + 1)]), ["d_mp", "r16"], ["g1_%d" % i])
    def slot_lookup(q, i):
        b = 2 * (i ^ (rank // 4 * 2))
        copy(q, T.g2[:, U * b:U * (b + 2)], T.g1[:].indirect(T.uc16[:, UC * b:UC * (b + 2)]), ["g1_0", "g1_1", "uc16"], ["g2_%d" % i])
    def turn(i):
        k, v = (i // 2) ^ (rank // 4), i % 2
        op("p", [lambda j=j: P.matmul(bank(6 + v, 0, 4 * UC), T.sel[:, 144 * v + 15 - j:144 * v + 143 - j],
                                      T.g2[:, 4 * U * k + j:4 * U * (k + 1):16], j == 0, j == 15) for j in range(16)],
           ["sel", "g2_%d" % (i - v), "g2_%d" % (i - v + 1)], ["B%d" % (6 + v)])
    def list_copy(q, i):
        k, v = (i // 2) ^ (rank // 4), i % 2
        a = N * UC * v + 4 * UC * k
        copy(q, T.l16[:, a:a + 4 * UC], bank(6 + v, 0, 4 * UC), ["B%d" % (6 + v)], ["l16_%d_%d" % (k, v)])

    def px_mm(j):
        matmul(bank(j % 6), T.bdb[:, 128 * (j // 4):128 * (j // 4 + 1)], T.xs[:, 512 * j:512 * (j + 1)],
               ["bdb", "d_x%d" % (j // 2)], ["B%d" % (j % 6)])
    def px_copy(q, j):
        copy(q, T.px[:, 512 * j:512 * (j + 1)], bank(j % 6), ["B%d" % (j % 6)], ["px%d" % j])

    zb = {role[c]: b for c, b in (("r1", 0), ("r2", 1), ("e2", 2), ("r3", 3), ("r4", 0), ("e4", 1))}
    p2 = T.raw[:, 0:128]
    def blk(buf, q):
        return buf[:, U * q:U * (q + 1)]
    def send(q, name):
        order("g", [name], [])
        trs = []
        for a, n, c, k, es in block_plan(cores, rank, topo)[q]:
            rid, pid = topo.addr(c, core)
            src, dst = (T.raw[:], T.lraw[:]) if q == role["e3"] else (T.zs[:, U * q + a:U * q + a + n], T.land[:, U * k:U * k + n])
            trs.append(RemoteDMATransfer(dst_ids=[DstId(rid=rid, pnc=pid)], dma_engine_mask=bits(es), remote_sem=T.sem["arr%d" % k],
                                         src=src, dst=dst))
            total["sent"] += len(es)
        g.remote_dma_fused(trs, local_sem=T.sem.sent)
    def a_op(e, q):
        copy(e, blk(T.ab, q), T.px[:, 0:C].indirect(T.l16[:, UC * q:UC * (q + 1)]),
             ["l16_%d_0" % (q // 4), "px0", "px1", "px2", "px3"], ["ab%d" % q])
    def b_op(q):
        out = blk(T.land, q) if q == rank else T.raw[:, 128:] if q == role["e3"] else blk(T.x2, q)
        name = ("land%d" if q == rank else "x2_%d") % q
        mult(out, T.px[:, C:2 * C].indirect(T.l16[:, UC * (N + q):UC * (N + q + 1)]), blk(T.ab, q),
             ["l16_%d_1" % (q // 4), "px4", "px5", "px6", "px7", "ab%d" % q], [name])
        if q in zb:
            matmul(bank(zb[q], 0, U), p2, out, ["p2", name], ["B%d" % zb[q]])
        elif q != rank:
            order("g", ["p2"], [])
            send(q, name)
    def z_op(e, q):
        copy(e, blk(T.zs, q), bank(zb[q], 0, U), ["B%d" % zb[q]], ["zs%d" % q])
        send(q, "zs%d" % q)

    top = {role["e1"]: 4, role["e3"]: 0}
    wbank = {"1e": 5, "1a": 2, "1b": 3, "2e": 1, "2a": 5, "2b": 2}
    def xe(r):
        return T.xe[:, TT * r:TT * (r + 1)]
    def expand(e, r):
        win = T.lraw[:, 128:] if r == role["e3"] else blk(T.land, r)
        copy(e, xe(r), win.indirect(T.po16[:, PC * (r ^ rank):PC * ((r ^ rank) + 1)]),
             ["land%d" % r, "po_own" if r == rank else "po16"], ["xe%d" % r])
        if r in top:
            matmul(bank(top[r]), p2 if r == rank else T.lraw[:, 0:128], xe(r), ["p2", "land%d" % r, "xe%d" % r], ["B%d" % top[r]])
    def join(name):
        x, e, a, b = [role[c] for c in ("e1 e2 r1 r2" if name[0] == "1" else "e3 e4 r3 r4").split()]
        y, c, d = {"e": (e, a, b), "a": (a, e, b), "b": (b, e, a)}[name[1]]
        h = (x, y) if 0 in (x % 4, y % 4) else (c, d)
        return 3 * (x // 4) + max(h[0] % 4, h[1] % 4) - 1, x, y, c, d
    def col(buf, j, a=0, n=TT):
        return buf[:, TT * j + a:TT * j + a + n]
    def m_step(name):
        j, x, y, c, d = join(name)
        mult(col(T.ll, j), xe(y), bank(top[x]), ["xe%d" % y, "B%d" % top[x]], ["l%d" % j])
        k = 1 if 0 in (x % 4, y % 4) else 0
        matmul(bank(wbank[name]), T.bdw[:, 128 * k:128 * (k + 1)], col(T.ll, j), ["w", "wt", "l%d" % j], ["B%d" % wbank[name]])
    def u_step(name):
        j, x, y, c, d = join(name)
        b = wbank[name]
        mult(bank(b), xe(c), bank(b), ["xe%d" % c, "B%d" % b], ["B%d" % b])
    def v_op(name, a=0, n=TT):
        j, x, y, c, d = join(name)
        b = wbank[name]
        mult(col(T.vv, j, a, n), xe(d)[:, a:a + n], bank(b, a, n), ["xe%d" % d, "B%d" % b],
             ["v%d_%d" % (j, i) for i in range(a // 128, (a + n) // 128)])
        return j
    summed = {"1": ["1e", "1a", "1b"], "2": ["2e", "2a"]}
    def v_step(name):
        j = v_op(name)
        i = (summed["1"] + summed["2"]).index(name)
        op("p", [lambda c=c: P.matmul(acc[:, 512 * 6 + 32 * i + c:512 * 6 + 32 * (i + 1):4], col(T.vv, j, 128 * c, 128),
                                      T.ones[:, 3:35:4], True, True) for c in range(4)],
           ["ones"] + ["v%d_%d" % (j, c) for c in range(4)], ["B6", "sum" + name])
    total["ydone"] = 0
    def store(j, p, a, name):
        order("y", [name], [])
        g.sync.dma_start(T.y[:, TT * j:TT * (j + 1)], T.ys[p:p + 32, a:a + 128]).then_inc(T.sem.ydone, 16)
        total["ydone"] += 16
    def turn_sums(e, k):
        n, a = 32 * len(summed[k]), int(k) - 1
        copy(e, T.rs[:, 96 * a:96 * a + n], bank(6, 96 * a, n), ["B6"] + ["sum" + j for j in summed[k]], ["rs" + k])
        op("p", [lambda: P.transpose(acc[0:n, 512 * 7:512 * 7 + 128], T.rs[:, 96 * a:96 * a + n], T.i32[:])],
           ["rs" + k, "i32"], ["B7"])
    def store_sums(e, k):
        n, a = 32 * len(summed[k]), int(k) - 1
        copy(e, T.ys[0:n, 128 * a:128 * (a + 1)], acc[0:n, 512 * 7:512 * 7 + 128], ["B7"], ["ys" + k])
        for i, name in enumerate(summed[k]):
            store(join(name)[0], 32 * i, 128 * a, "ys" + k)
    def last():
        for a, n in ((0, 2), (2, 1), (3, 1)):
            j = v_op("2b", 128 * a, 128 * n)
            op("p", [lambda c=c: P.matmul(acc[0:32, 2048:2176], T.ones[:, 3 - c:35 - c], col(T.vv, j, 128 * c, 128), c == 0, c == 3)
                     for c in range(a, a + n)], ["ones"] + ["v%d_%d" % (j, c) for c in range(a, a + n)], ["B4"])
        copy("s", T.ys[0:32, 256:384], acc[0:32, 2048:2176], ["B4"], ["ys3"])
        store(j, 0, 256, "ys3")
    def constants():
        scalar(T.ic2[:], T.ic[:], 4, ALU.arith_shift_right, ["ic"], ["ic2"])
        scalar(T.i32[:], T.ii[:], 0.0, ALU.is_equal, ["ii"], ["i32"])
        scalar(T.ones[:], T.ic2[:], 8.0, ALU.is_equal, ["ic2"], ["ones"])
    def diag(q, out, a, n, name):
        copy(q, out, T.trz[:, 0:80].indirect(T.bdo[:, a:a + n]), ["d_tr", "trz", "bdo"], [name])
    def w_turned(e):
        matmul(bank(7, 0, 128), T.bdw[:, 0:128], T.i32[:], ["w", "i32"], ["B7"])
        copy(e, T.bdw[:, 128:256], bank(7, 0, 128), ["B7"], ["wt"])

    step = {"bdb": lambda: diag("s", T.bdb[:], 0, 16, "bdb"), "cst": constants, "end": last,
            "sel": lambda: scalar(T.sel[:], T.ie[:], 0.0, ALU.is_equal, ["ie"], ["sel"])}
    by_queue = {
        "p2": lambda e: diag(e, p2, 16, 8, "p2"), "w": lambda e: diag(e, T.bdw[:, 0:128], 24, 8, "w"), "wt": w_turned,
        "r": lambda e: copy(e, T.r16[:], T.rep32[:], ["d_rep"], ["r16"]),
        "uc": lambda e: copy(e, T.uc16[:], T.uc32[:], ["d_uc"], ["uc16"]),
        "po": lambda e: copy(e, T.po16[:, PC:], T.psl[:, PC:], ["psl"], ["po16"]),
        "o": lambda e: copy(e, T.po16[:, 0:PC], T.ps32[:, PC * rank:PC * (rank + 1)], ["d_ps"], ["po_own"]),
    }
    by_number = {"p": px_copy, "g": lookup, "G": slot_lookup, "l": list_copy}
    by_name = {"a": a_op, "z": z_op, "x": expand, "f": turn_sums, "y": store_sums}
    alone = {"b": b_op, "m": m_step, "u": u_step, "v": v_step}
    for s in OPT["sched"]:
        f, dot, w = s.partition(".")
        if s in step:
            step[s]()
        elif dot and f in alone:
            alone[f](role.get(w, w))
        elif dot:
            by_name[f[0]](f[1], role.get(w, w))
        elif s[:-1] in by_queue:
            by_queue[s[:-1]](s[-1])
        elif s[:-1] == "pm":
            px_mm(int(s[-1]))
        elif s[0] == "t":
            turn(int(s[1]))
        else:
            by_number[s[0]](s[1], int(s[2]))

    for s in total:
        if s != "ydone" and max(waited[q].get(s, 0) for q in waited) < total[s]:
            wait("g", s, total[s])
    wait("y", "ydone", total["ydone"])
